import numpy as np
import ml_dtypes


def mxq(x, axis, fmt="e4m3"):
    dtype, down = {"e4m3": (ml_dtypes.float8_e4m3fn, 7), "e5m2": (ml_dtypes.float8_e5m2, 14)}[fmt]
    v = np.moveaxis(np.asarray(x, np.float32).astype(ml_dtypes.bfloat16).astype(np.float64), axis, -1)
    blocks = v.reshape(v.shape[:-1] + (-1, 32))
    amax = np.abs(blocks).max(-1, keepdims=True)
    byte = np.maximum(np.where(amax > 0, np.frexp(amax)[1] - 1 + 127, 0) - down, 1)
    scale = np.exp2(byte - 127.0)
    codes = (blocks / scale).astype(np.float32).astype(dtype).astype(np.float64)
    return np.moveaxis((codes * scale).reshape(v.shape), -1, axis)


WIDE = False


def mx_kscale(k):
    if not WIDE:
        return np.ones(k)
    levels = np.array([30, -30])
    if k % 512:
        return np.exp2(np.random.permutation(np.resize(levels, k // 32))).repeat(32)
    a = np.empty((k // 512, 16))
    for p in range(k // 512):
        a[p, :8] = np.random.permutation(np.resize(levels, 8))
        for g in range(8):
            far = levels[np.abs(levels - a[p, g]) >= 10]
            a[p, g + 8] = far[np.random.randint(len(far))]
    return np.exp2(a.ravel()).repeat(32)


BF16 = ml_dtypes.bfloat16


def bf(x):
    return np.asarray(x, np.float32).astype(BF16)


def f64(x):
    return np.asarray(x).astype(np.float64)


E2M1 = np.array([0.0, 0.5, 1.0, 1.5, 2.0, 3.0, 4.0, 6.0, -0.0, -0.5, -1.0, -1.5, -2.0, -3.0, -4.0, -6.0])


def pack_weight(w, fmt):
    k, n = w.shape
    w = f64(bf(w)).reshape(k // 32, 32, n)
    amax = np.abs(w).max(1)
    if fmt == "e4m3":
        byte = np.frexp(amax)[1] - 1 + 127 - 7
    else:
        mant, ex = np.frexp(amax / 6.0)
        byte = np.where(mant > 0.5, ex, ex - 1) + 127
    byte = np.clip(np.where(amax > 0, byte, 1), 1, 254)
    scaled = (w * np.exp2(127.0 - byte)[:, None, :]).reshape(k, n).astype(np.float32)
    by_word = np.ascontiguousarray(scaled.reshape(k // 512, 128, 4, n).transpose(0, 1, 3, 2))
    if fmt == "e4m3":
        words = by_word.astype(ml_dtypes.float8_e4m3fn).view(np.uint8)
    else:
        c = by_word.astype(ml_dtypes.float4_e2m1fn).view(np.uint8) & 0xF
        words = c[..., 0::2] | (c[..., 1::2] << 4)
    return np.ascontiguousarray(words), np.ascontiguousarray(byte.astype(np.uint8).reshape(k // 512, 16, n))


def unpack_weight(words, scales, fmt):
    g, p, n, _ = words.shape
    if fmt == "e4m3":
        vals = np.ascontiguousarray(words).view(ml_dtypes.float8_e4m3fn).astype(np.float64)
    else:
        nib = np.empty((g, p, n, 4), np.uint8)
        nib[..., 0::2] = words & 0xF
        nib[..., 1::2] = words >> 4
        vals = E2M1[nib]
    vals = vals * np.repeat(np.exp2(scales.astype(np.float64) - 127.0), 8, axis=1)[..., None]
    return vals.transpose(0, 1, 3, 2).reshape(g * 512, n)
def pack4(w):
    words, scales = pack_weight(w, "e2m1")
    return words.reshape(words.shape[0], 128, -1), scales


def unpack4(words, scales):
    return unpack_weight(words.reshape(words.shape[0], 128, -1, 2), scales, "e2m1")


T, D, L, H, E = 1024, 2048, 1024, 1024, 1536


def setup_inputs():
    s, t = mx_kscale(D), mx_kscale(L)
    x = np.random.standard_normal((T, D)) * s
    down = np.random.standard_normal((D, L)) / np.sqrt(D) / s[:, None]
    down_words, down_scales = pack4(down)
    return {
        "x": bf(x),
        "down_words": down_words,
        "down_scales": down_scales,
        "gain": bf((1 + 0.1 * np.random.standard_normal(L)) * t),
        "shift": bf(0.3 * np.random.standard_normal(L) * t),
        "wk": bf(np.random.standard_normal((L, H)) / np.sqrt(L) / t[:, None]),
        "bk": bf(0.3 * np.random.standard_normal(H)),
        "wv": bf(np.random.standard_normal((L, E)) / np.sqrt(L) / t[:, None]),
    }


def reference(x, down_words, down_scales, gain, shift, wk, bk, wv):
    z = mxq(f64(x), 1, "e4m3") @ unpack4(down_words, down_scales)
    c = z * f64(gain) + f64(shift)
    cq = mxq(c, 1, "e5m2")
    keys = (mxq(f64(wk), 0, "e4m3").T @ cq.T) + f64(bk)[:, None]
    values = cq @ mxq(f64(wv), 0, "e4m3")
    return keys, values

@@ -1,0 +1,353 @@
+from contextlib import ExitStack
+
+import concourse.mybir as mybir
+from concourse.masks import make_identity
+
+T, D, L, H, E = 1024, 2048, 1024, 1024, 1536
+FLOPS = 2 * T * D * L + 2 * T * L * (H + E)
+
+F32 = mybir.dt.float32
+BF16 = mybir.dt.bfloat16
+I32 = mybir.dt.int32
+U32 = mybir.dt.uint32
+U8 = mybir.dt.uint8
+E4M3 = mybir.dt.float8_e4m3fn_x4
+E5M2 = mybir.dt.float8_e5m2_x4
+E2M1 = mybir.dt.float4_e2m1fn_x4
+IDENTITY = mybir.ActivationFunctionType.Identity
+MULT = mybir.AluOpType.mult
+ADD = mybir.AluOpType.add
+
+P = 128
+PACK = 4
+KP = P * PACK
+N = 512
+HALVES = T // N
+D_PASSES = D // KP
+L_PASSES = L // KP
+TILES = N // P
+RUN = 4
+
+
+def tile_latent_key_value_cache_s9_kernel(tc, x, down_words, down_scales, gain, shift, wk, bk, wv, keys, values):
+    nc = tc.nc
+    with ExitStack() as ctx:
+        keep = ctx.enter_context(tc.tile_pool(name="keep", bufs=1))
+        stage = ctx.enter_context(tc.tile_pool(name="stage", bufs=4))
+        psum = ctx.enter_context(tc.psum_pool(name="psum", bufs=1))
+        ctx.enter_context(tc.manual_schedule())
+
+        def kept(name, shape, dtype):
+            return keep.tile(shape, dtype, name=name, align_bytes=64)
+
+        def bank(b, shape):
+            return psum.tile(shape, F32, name="bank%d" % b)
+
+        ident = kept("ident", [P, P], F32)
+        make_identity(nc, ident[:])
+        scale_raw = kept("scale_raw", [P, D_PASSES * L], U8)
+        nc.vector.memset(scale_raw[:].bitcast(I32), 0)
+        rows32 = kept("rows32", [P, N], F32)
+        nc.vector.memset(rows32[:], 0.0)
+        warm = kept("warm", [P, 1], F32)
+        nc.scalar.activation(out=warm[:], in_=rows32[:, 0:1], func=IDENTITY)
+
+        x_raw, w_raw, wk_raw, wv_raw = {}, {}, {}, {}
+
+        def load_x(h, g):
+            x_raw[h, g] = kept("x_raw%d%d" % (h, g), [P, TILES, KP], BF16)
+            src = x[h * N:(h + 1) * N, g * KP:(g + 1) * KP].rearrange("(i p) k -> p i k", p=P)
+            nc.sync.dma_start(out=x_raw[h, g][:], in_=src)
+
+        def load_w(g):
+            w_raw[g] = kept("w_raw%d" % g, [P, 2 * L], U8)
+            nc.sync.dma_start(out=w_raw[g][:].bitcast(I32), in_=down_words[g].bitcast(I32))
+
+        def load_second_weight(raw, name, weight, c):
+            raw[c] = kept("%s%d" % (name, c), [P, PACK, weight.shape[1]], BF16)
+            rows = weight[c * KP:(c + 1) * KP, :].rearrange("(m t b) n -> b m t n", t=PACK, b=RUN)
+            for b in range(RUN):
+                nc.sync.dma_start(out=raw[c][b:P:RUN, :, :], in_=rows[b])
+
+        load_x(0, 0)
+        load_x(0, 1)
+        for r in range(4):
+            nc.sync.dma_start(
+                out=scale_raw[r:P:32, :].bitcast(I32).rearrange("q (g n) -> q g n", g=D_PASSES),
+                in_=down_scales[:, r:16:4, :].bitcast(I32).rearrange("g q n -> q g n"))
+        load_w(0)
+        load_w(1)
+        load_x(0, 2)
+        load_w(2)
+        load_x(0, 3)
+        load_w(3)
+        rows16 = kept("rows16", [P, N], BF16)
+        nc.sync.dma_start(out=rows16[0:2, :], in_=gain.rearrange("(c n) -> c n", n=N))
+        nc.sync.dma_start(out=rows16[2:4, :], in_=shift.rearrange("(c n) -> c n", n=N))
+        nc.sync.dma_start(out=rows16[32:34, :], in_=bk.rearrange("(c n) -> c n", n=N))
+        load_second_weight(wk_raw, "wk_raw", wk, 0)
+        load_second_weight(wk_raw, "wk_raw", wk, 1)
+        for g in range(D_PASSES):
+            load_x(1, g)
+        load_second_weight(wv_raw, "wv_raw", wv, 0)
+        load_second_weight(wv_raw, "wv_raw", wv, 1)
+
+        w_codes, w_scales = {}, {}
+
+        def permute_w(g):
+            w_scales[g] = kept("w_scales%d" % g, [P, L], U8)
+            nc.vector.tensor_copy(
+                out=w_scales[g][:].bitcast(I32).rearrange("p (c t a m) -> p c a t m", c=L_PASSES, t=PACK, m=4),
+                in_=scale_raw[:, g * L:(g + 1) * L].bitcast(I32).rearrange("p (c a m t) -> p c a t m", c=L_PASSES, t=PACK, m=4))
+            w_codes[g] = kept("w_codes%d" % g, [P, 2 * L], U8)
+            nc.vector.tensor_copy(
+                out=w_codes[g][:].bitcast(I32).rearrange("p (c t m w) -> p c t m w", c=L_PASSES, t=PACK, w=2),
+                in_=w_raw[g][:].bitcast(I32).rearrange("p (c m t w) -> p c t m w", c=L_PASSES, t=PACK, w=2))
+
+        turned, grouped, quantised = {}, {}, {}
+
+        def transpose_x(h, g, banks):
+            for pair in range(2):
+                turned[h, g, pair] = bank(banks[pair], [P, 2, 2, P])
+                for i in range(2):
+                    words = x_raw[h, g][:, 2 * pair + i, :].bitcast(F32)
+                    for u in range(2):
+                        nc.tensor.transpose(turned[h, g, pair][:, i, u, :], words[:, u:KP // 2:2], ident[:])
+
+        def new_grouped(key):
+            grouped[key] = stage.tile([P, PACK * N], BF16, name="grouped", align_bytes=64)
+
+        def empty_x(h, g, pair, copy):
+            if pair == 0:
+                new_grouped(("x", h, g))
+            dst = grouped["x", h, g][:, pair * 2 * N:(pair + 1) * 2 * N].bitcast(F32)
+            copy(out=dst.rearrange("p (i r u) -> p i r u", i=2, u=2), in_=turned[h, g, pair][:].rearrange("p i u r -> p i r u"))
+
+        def interleave(key, src, copy):
+            new_grouped(key)
+            copy(out=grouped[key][:].rearrange("p (c i t) -> p c t i", t=PACK, i=4),
+                 in_=src.rearrange("p t (c i) -> p c t i", i=4))
+
+        def quantise(key, fmt):
+            name = "_".join(str(k) for k in key)
+            codes = kept("codes_" + name, [P, N], U32)
+            scales = kept("scales_" + name, [P, N], U8)
+            nc.vector.quantize_mx(out=codes[:].bitcast(fmt), scales=scales[:], in_=grouped[key][:])
+            quantised[key] = (codes, scales)
+
+        consts = kept("consts", [P, PACK, 64], F32)
+
+        def widen_consts():
+            nc.vector.tensor_copy(out=rows32[0:4, :].rearrange("p (t m b) -> p t m b", t=PACK, b=RUN),
+                                  in_=rows16[0:4, :].rearrange("p (m t b) -> p t m b", t=PACK, b=RUN))
+            nc.vector.tensor_copy(out=rows32[32:34, :], in_=rows16[32:34, :])
+
+        def make_consts(b):
+            cols = bank(b, [P, PACK, P])
+            for t in range(PACK):
+                nc.tensor.transpose(cols[:, t, :], rows32[:, t * P:(t + 1) * P], ident[:])
+            nc.scalar.copy(out=consts[:], in_=cols[:, :, 0:64])
+
+        z, latent = {}, {}
+
+        def down_pass(h, c, t, g, b):
+            if g == 0:
+                z[h, c, t] = bank(b, [P, N])
+            col = c * KP + t * P
+            codes, scales = quantised["x", h, g]
+            nc.tensor.matmul_mx(
+                out=z[h, c, t][:],
+                lhsT=w_codes[g][:, 2 * col:2 * (col + P)].bitcast(E2M1), lhsT_scale=w_scales[g][:, col:col + P],
+                rhs=codes[:].bitcast(E4M3), rhs_scale=scales[:], start=(g == 0), stop=(g == D_PASSES - 1))
+
+        def empty_z(h, c, t, on_scalar=True):
+            if t == 0:
+                latent[h, c] = stage.tile([P, PACK, N], BF16, name="latent", bufs=2, align_bytes=64)
+            g_col, s_col = consts[:, t, c:c + 1], consts[:, t, 2 + c:3 + c]
+            if on_scalar:
+                nc.scalar.activation(out=latent[h, c][:, t, :], in_=z[h, c, t][:], func=IDENTITY, scale=g_col, bias=s_col)
+            else:
+                nc.vector.tensor_scalar(out=latent[h, c][:, t, :], in0=z[h, c, t][:], scalar1=g_col, scalar2=s_col, op0=MULT, op1=ADD)
+
+        acc = {}
+
+        def keys_pass(h, j, c, b):
+            if c == 0:
+                acc["k", h, j] = bank(b, [P, N])
+            wc, ws = quantised["wk", c, j // TILES]
+            cc, cs = quantised["c", h, c]
+            cols = slice((j % TILES) * P, (j % TILES + 1) * P)
+            nc.tensor.matmul_mx(out=acc["k", h, j][:], lhsT=wc[:, cols].bitcast(E4M3), lhsT_scale=ws[:, cols],
+                                rhs=cc[:].bitcast(E5M2), rhs_scale=cs[:], start=(c == 0), stop=(c == L_PASSES - 1))
+
+        def values_pass(h, e, i, c, b):
+            if c == 0:
+                acc["v", h, e, i] = bank(b, [P, N])
+            wc, ws = quantised["wv", c, e]
+            cc, cs = quantised["c", h, c]
+            cols = slice(i * P, (i + 1) * P)
+            nc.tensor.matmul_mx(out=acc["v", h, e, i][:], lhsT=cc[:, cols].bitcast(E5M2), lhsT_scale=cs[:, cols],
+                                rhs=wc[:].bitcast(E4M3), rhs_scale=ws[:], start=(c == 0), stop=(c == L_PASSES - 1))
+
+        def finish_keys(h, j, on_scalar):
+            out = stage.tile([P, N], F32, name="result", bufs=14)
+            bias = consts[:, j % PACK, 32 + j // PACK:33 + j // PACK]
+            if on_scalar:
+                nc.scalar.activation(out=out[:], in_=acc["k", h, j][:], func=IDENTITY, bias=bias)
+            else:
+                nc.vector.tensor_scalar(out=out[:], in0=acc["k", h, j][:], scalar1=bias, scalar2=None, op0=ADD)
+            nc.sync.dma_start(out=keys[j * P:(j + 1) * P, h * N:(h + 1) * N], in_=out[:])
+
+        def finish_values(h, e, i, on_scalar):
+            out = stage.tile([P, N], F32, name="result", bufs=14)
+            copy = nc.scalar.copy if on_scalar else nc.vector.tensor_copy
+            copy(out=out[:], in_=acc["v", h, e, i][:])
+            row = h * N + i * P
+            nc.sync.dma_start(out=values[row:row + P, e * N:(e + 1) * N], in_=out[:])
+
+        S, V = nc.scalar.copy, nc.vector.tensor_copy
+
+        def prep(kind, c, chunk, copy=V):
+            raw = wk_raw if kind == "wk" else wv_raw
+            interleave((kind, c, chunk), raw[c][:, :, chunk * N:(chunk + 1) * N], copy)
+
+        def q4(*key):
+            quantise(key, E4M3)
+
+
+        A, B = [0, 1, 2, 3], [4, 5, 6, 7]
+
+        def keys_job(h, j, b, on_scalar):
+            for c in range(L_PASSES):
+                keys_pass(h, j, c, b)
+            finish_keys(h, j, on_scalar)
+
+        def values_job(h, e, i, b, on_scalar):
+            for c in range(L_PASSES):
+                values_pass(h, e, i, c, b)
+            finish_values(h, e, i, on_scalar)
+
+        def down_group(h, c, t, b):
+            for g in range(D_PASSES):
+                down_pass(h, c, t, g, b)
+
+        transpose_x(0, 0, B[0:2])
+        empty_x(0, 0, 0, S)
+        empty_x(0, 0, 1, V)
+        transpose_x(0, 1, B[2:4])
+        empty_x(0, 1, 0, S)
+        q4("x", 0, 0)
+        empty_x(0, 1, 1, S)
+        permute_w(0)
+        for t in range(4):
+            down_pass(0, 0, t, 0, A[t])
+        permute_w(1)
+        transpose_x(0, 2, B[0:2])
+        q4("x", 0, 1)
+        empty_x(0, 2, 0, S)
+        empty_x(0, 2, 1, V)
+        for t in range(4):
+            down_pass(0, 0, t, 1, A[t])
+        permute_w(2)
+        widen_consts()
+        transpose_x(0, 3, B[2:4])
+        q4("x", 0, 2)
+        empty_x(0, 3, 0, S)
+        empty_x(0, 3, 1, V)
+        make_consts(B[1])
+        permute_w(3)
+        for t in range(4):
+            down_pass(0, 0, t, 2, A[t])
+        q4("x", 0, 3)
+        for g in range(3):
+            down_pass(0, 1, 0, g, B[0])
+        prep("wk", 0, 0)
+        prep("wk", 0, 1)
+        for t in range(4):
+            down_pass(0, 0, t, 3, A[t])
+            empty_z(0, 0, t)
+        q4("wk", 0, 0)
+        q4("wk", 0, 1)
+        down_pass(0, 1, 0, 3, B[0])
+        empty_z(0, 1, 0)
+        prep("wk", 1, 0)
+        down_group(0, 1, 1, B[1])
+        empty_z(0, 1, 1)
+        interleave(("c", 0, 0), latent[0, 0][:], V)
+        q4("wk", 1, 0)
+        down_group(0, 1, 2, B[2])
+        empty_z(0, 1, 2)
+        quantise(("c", 0, 0), E5M2)
+        transpose_x(1, 0, A[0:2])
+        empty_x(1, 0, 0, S)
+        empty_x(1, 0, 1, V)
+        transpose_x(1, 1, A[2:4])
+        empty_x(1, 1, 0, S)
+        q4("x", 1, 0)
+        down_group(0, 1, 3, B[3])
+        empty_x(1, 1, 1, V)
+        empty_z(0, 1, 3)
+        prep("wk", 1, 1)
+        for t in range(4):
+            down_pass(1, 0, t, 0, B[t])
+        transpose_x(1, 2, A[0:2])
+        q4("x", 1, 1)
+        interleave(("c", 0, 1), latent[0, 1][:], V)
+        q4("wk", 1, 1)
+        empty_x(1, 2, 0, S)
+        empty_x(1, 2, 1, S)
+        for t in range(4):
+            down_pass(1, 0, t, 1, B[t])
+        transpose_x(1, 3, A[2:4])
+        q4("x", 1, 2)
+        quantise(("c", 0, 1), E5M2)
+        empty_x(1, 3, 0, S)
+        empty_x(1, 3, 1, S)
+        prep("wv", 0, 0)
+        for t in range(4):
+            down_pass(1, 0, t, 2, B[t])
+        q4("x", 1, 3)
+        q4("wv", 0, 0)
+        keys_job(0, 0, A[0], True)
+        keys_job(0, 1, A[1], True)
+        prep("wv", 1, 0)
+        prep("wv", 0, 1)
+        for t in range(4):
+            down_pass(1, 0, t, 3, B[t])
+            empty_z(1, 0, t)
+        q4("wv", 1, 0)
+        q4("wv", 0, 1)
+        down_group(1, 1, 0, A[2])
+        keys_job(0, 2, A[3], True)
+        keys_job(0, 3, A[0], True)
+        prep("wv", 1, 1)
+        interleave(("c", 1, 0), latent[1, 0][:], V)
+        down_group(1, 1, 1, A[1])
+        empty_z(1, 1, 0)
+        keys_job(0, 4, B[0], True)
+        empty_z(1, 1, 1)
+        keys_job(0, 5, B[1], True)
+        q4("wv", 1, 1)
+        quantise(("c", 1, 0), E5M2)
+        down_group(1, 1, 2, B[2])
+        prep("wv", 0, 2)
+        prep("wv", 1, 2)
+        empty_z(1, 1, 2)
+        keys_job(0, 6, B[3], True)
+        keys_job(0, 7, A[2], True)
+        q4("wv", 0, 2)
+        q4("wv", 1, 2)
+        down_group(1, 1, 3, A[3])
+        empty_z(1, 1, 3)
+        ring = [A[0], A[1], B[0], B[1], B[2], B[3], A[2], A[3]]
+        jobs = [("v", 0, e, i) for e in range(3) for i in range(4)] + [("k", 1, j) for j in range(8)] + [("v", 1, e, i) for e in range(3) for i in range(4)]
+        for step, job in enumerate(jobs):
+            if step == 2:
+                interleave(("c", 1, 1), latent[1, 1][:], V)
+            if step == 6:
+                quantise(("c", 1, 1), E5M2)
+            on_scalar = step % 2 == 0 or step == 3
+            if job[0] == "k":
+                keys_job(job[1], job[2], ring[step % 8], on_scalar)
+            else:
+                values_job(job[1], job[2], job[3], ring[step % 8], on_scalar)

@@ -45,8 +45,10 @@ def tile_latent_key_value_cache_s9_kernel(tc, x, down_words, down_scales, gain, 
 
         ident = kept("ident", [P, P], F32)
         make_identity(nc, ident[:])
-        scale_raw = kept("scale_raw", [P, D_PASSES * L], U8)
-        nc.vector.memset(scale_raw[:].bitcast(I32), 0)
+        scale_raw = {}
+        for c in range(L_PASSES):
+            scale_raw[c] = kept("scale_raw%d" % c, [P, D_PASSES * KP // 4], I32)
+            nc.vector.memset(scale_raw[c][:], 0)
         rows32 = kept("rows32", [P, N], F32)
         nc.vector.memset(rows32[:], 0.0)
         warm = kept("warm", [P, 1], F32)
@@ -54,14 +56,24 @@ def tile_latent_key_value_cache_s9_kernel(tc, x, down_words, down_scales, gain, 
 
         x_raw, w_raw, wk_raw, wv_raw = {}, {}, {}, {}
 
-        def load_x(h, g):
-            x_raw[h, g] = kept("x_raw%d%d" % (h, g), [P, TILES, KP], BF16)
-            src = x[h * N:(h + 1) * N, g * KP:(g + 1) * KP].rearrange("(i p) k -> p i k", p=P)
-            nc.sync.dma_start(out=x_raw[h, g][:], in_=src)
+        def load_x(h, g, pairs=(0, 1)):
+            raw = kept("x_raw%d%d%d" % (h, g, pairs[0]), [P, 2 * len(pairs), KP], BF16)
+            row = h * N + pairs[0] * 2 * P
+            src = x[row:row + len(pairs) * 2 * P, g * KP:(g + 1) * KP].rearrange("(i p) k -> p i k", p=P)
+            nc.sync.dma_start(out=raw[:], in_=src)
+            for n, pair in enumerate(pairs):
+                x_raw[h, g, pair] = raw[:, 2 * n:2 * n + 2, :]
 
-        def load_w(g):
-            w_raw[g] = kept("w_raw%d" % g, [P, 2 * L], U8)
-            nc.sync.dma_start(out=w_raw[g][:].bitcast(I32), in_=down_words[g].bitcast(I32))
+        def load_w(c, g0, g1):
+            w_raw[c, g0] = kept("w_raw%d%d" % (c, g0), [P, g1 - g0, KP // 2], I32)
+            src = down_words[g0:g1, :, 2 * c * KP:2 * (c + 1) * KP].bitcast(I32).rearrange("g p n -> p g n")
+            nc.sync.dma_start(out=w_raw[c, g0][:], in_=src)
+
+        def load_w_scales(c):
+            for r in range(4):
+                nc.sync.dma_start(
+                    out=scale_raw[c][r:P:32, :].rearrange("q (g n) -> q g n", g=D_PASSES),
+                    in_=down_scales[:, r:16:4, c * KP:(c + 1) * KP].bitcast(I32).rearrange("g q n -> q g n"))
 
         def load_second_weight(raw, name, weight, c):
             raw[c] = kept("%s%d" % (name, c), [P, PACK, weight.shape[1]], BF16)
@@ -69,22 +81,20 @@ def tile_latent_key_value_cache_s9_kernel(tc, x, down_words, down_scales, gain, 
             for b in range(RUN):
                 nc.sync.dma_start(out=raw[c][b:P:RUN, :, :], in_=rows[b])
 
-        load_x(0, 0)
+        load_x(0, 0, (0,))
+        load_x(0, 0, (1,))
         load_x(0, 1)
-        for r in range(4):
-            nc.sync.dma_start(
-                out=scale_raw[r:P:32, :].bitcast(I32).rearrange("q (g n) -> q g n", g=D_PASSES),
-                in_=down_scales[:, r:16:4, :].bitcast(I32).rearrange("g q n -> q g n"))
-        load_w(0)
-        load_w(1)
+        load_w_scales(0)
+        load_w(0, 0, 2)
         load_x(0, 2)
-        load_w(2)
-        load_x(0, 3)
-        load_w(3)
         rows16 = kept("rows16", [P, N], BF16)
         nc.sync.dma_start(out=rows16[0:2, :], in_=gain.rearrange("(c n) -> c n", n=N))
         nc.sync.dma_start(out=rows16[2:4, :], in_=shift.rearrange("(c n) -> c n", n=N))
         nc.sync.dma_start(out=rows16[32:34, :], in_=bk.rearrange("(c n) -> c n", n=N))
+        load_w(0, 2, 4)
+        load_x(0, 3)
+        load_w_scales(1)
+        load_w(1, 0, 4)
         load_second_weight(wk_raw, "wk_raw", wk, 0)
         load_second_weight(wk_raw, "wk_raw", wk, 1)
         for g in range(D_PASSES):
@@ -94,25 +104,32 @@ def tile_latent_key_value_cache_s9_kernel(tc, x, down_words, down_scales, gain, 
 
         w_codes, w_scales = {}, {}
 
-        def permute_w(g):
-            w_scales[g] = kept("w_scales%d" % g, [P, L], U8)
+        def permute_scales(c):
+            w_scales[c] = kept("w_scales%d" % c, [P, D_PASSES * KP], U8)
             nc.vector.tensor_copy(
-                out=w_scales[g][:].bitcast(I32).rearrange("p (c t a m) -> p c a t m", c=L_PASSES, t=PACK, m=4),
-                in_=scale_raw[:, g * L:(g + 1) * L].bitcast(I32).rearrange("p (c a m t) -> p c a t m", c=L_PASSES, t=PACK, m=4))
-            w_codes[g] = kept("w_codes%d" % g, [P, 2 * L], U8)
-            nc.vector.tensor_copy(
-                out=w_codes[g][:].bitcast(I32).rearrange("p (c t m w) -> p c t m w", c=L_PASSES, t=PACK, w=2),
-                in_=w_raw[g][:].bitcast(I32).rearrange("p (c m t w) -> p c t m w", c=L_PASSES, t=PACK, w=2))
+                out=w_scales[c][:].bitcast(I32).rearrange("p (g t a m) -> p g a t m", g=D_PASSES, t=PACK, m=4),
+                in_=scale_raw[c][:].rearrange("p (g a m t) -> p g a t m", g=D_PASSES, t=PACK, m=4))
 
-        turned, grouped, quantised = {}, {}, {}
+        def permute_codes(c, g0, g1):
+            codes = kept("w_codes%d%d" % (c, g0), [P, (g1 - g0) * 2 * KP], U8)
+            nc.vector.tensor_copy(
+                out=codes[:].bitcast(I32).rearrange("p (g t m w) -> p g t m w", g=g1 - g0, t=PACK, w=2),
+                in_=w_raw[c, g0][:].rearrange("p g (m t w) -> p g t m w", t=PACK, w=2))
+            for g in range(g0, g1):
+                w_codes[c, g] = codes[:, (g - g0) * 2 * KP:(g - g0 + 1) * 2 * KP]
+
+        sorted_x, turned, grouped, quantised = {}, {}, {}, {}
+
+        def sort_x(h, g, pair, copy):
+            sorted_x[h, g, pair] = stage.tile([P, 2, 2, P], F32, name="sorted_x", bufs=6, align_bytes=64)
+            copy(out=sorted_x[h, g, pair][:], in_=x_raw[h, g, pair].bitcast(F32).rearrange("p i (m u) -> p i u m", u=2))
 
         def transpose_x(h, g, banks):
             for pair in range(2):
                 turned[h, g, pair] = bank(banks[pair], [P, 2, 2, P])
                 for i in range(2):
-                    words = x_raw[h, g][:, 2 * pair + i, :].bitcast(F32)
                     for u in range(2):
-                        nc.tensor.transpose(turned[h, g, pair][:, i, u, :], words[:, u:KP // 2:2], ident[:])
+                        nc.tensor.transpose(turned[h, g, pair][:, i, u, :], sorted_x[h, g, pair][:, i, u, :], ident[:])
 
         def new_grouped(key):
             grouped[key] = stage.tile([P, PACK * N], BF16, name="grouped", align_bytes=64)
@@ -138,9 +155,9 @@ def tile_latent_key_value_cache_s9_kernel(tc, x, down_words, down_scales, gain, 
         consts = kept("consts", [P, PACK, 64], F32)
 
         def widen_consts():
-            nc.vector.tensor_copy(out=rows32[0:4, :].rearrange("p (t m b) -> p t m b", t=PACK, b=RUN),
+            nc.scalar.copy(out=rows32[0:4, :].rearrange("p (t m b) -> p t m b", t=PACK, b=RUN),
                                   in_=rows16[0:4, :].rearrange("p (m t b) -> p t m b", t=PACK, b=RUN))
-            nc.vector.tensor_copy(out=rows32[32:34, :], in_=rows16[32:34, :])
+            nc.scalar.copy(out=rows32[32:34, :], in_=rows16[32:34, :])
 
         def make_consts(b):
             cols = bank(b, [P, PACK, P])
@@ -153,11 +170,11 @@ def tile_latent_key_value_cache_s9_kernel(tc, x, down_words, down_scales, gain, 
         def down_pass(h, c, t, g, b):
             if g == 0:
                 z[h, c, t] = bank(b, [P, N])
-            col = c * KP + t * P
             codes, scales = quantised["x", h, g]
             nc.tensor.matmul_mx(
                 out=z[h, c, t][:],
-                lhsT=w_codes[g][:, 2 * col:2 * (col + P)].bitcast(E2M1), lhsT_scale=w_scales[g][:, col:col + P],
+                lhsT=w_codes[c, g][:, 2 * t * P:2 * (t + 1) * P].bitcast(E2M1),
+                lhsT_scale=w_scales[c][:, g * KP + t * P:g * KP + (t + 1) * P],
                 rhs=codes[:].bitcast(E4M3), rhs_scale=scales[:], start=(g == 0), stop=(g == D_PASSES - 1))
 
         def empty_z(h, c, t, on_scalar=True):
@@ -189,21 +206,48 @@ def tile_latent_key_value_cache_s9_kernel(tc, x, down_words, down_scales, gain, 
             nc.tensor.matmul_mx(out=acc["v", h, e, i][:], lhsT=cc[:, cols].bitcast(E5M2), lhsT_scale=cs[:, cols],
                                 rhs=wc[:].bitcast(E4M3), rhs_scale=ws[:], start=(c == 0), stop=(c == L_PASSES - 1))
 
-        def finish_keys(h, j, on_scalar):
-            out = stage.tile([P, N], F32, name="result", bufs=14)
+        def new_result(count):
+            return stage.tile([P, count, N], F32, name="result", bufs=7)
+
+        def empty_keys(h, j, out, on_scalar):
             bias = consts[:, j % PACK, 32 + j // PACK:33 + j // PACK]
             if on_scalar:
-                nc.scalar.activation(out=out[:], in_=acc["k", h, j][:], func=IDENTITY, bias=bias)
+                nc.scalar.activation(out=out, in_=acc["k", h, j][:], func=IDENTITY, bias=bias)
             else:
-                nc.vector.tensor_scalar(out=out[:], in0=acc["k", h, j][:], scalar1=bias, scalar2=None, op0=ADD)
-            nc.sync.dma_start(out=keys[j * P:(j + 1) * P, h * N:(h + 1) * N], in_=out[:])
+                nc.vector.tensor_scalar(out=out, in0=acc["k", h, j][:], scalar1=bias, scalar2=None, op0=ADD)
 
-        def finish_values(h, e, i, on_scalar):
-            out = stage.tile([P, N], F32, name="result", bufs=14)
+        def store_keys(h, j, count, out):
+            dst = keys[j * P:(j + count) * P, h * N:(h + 1) * N].rearrange("(j p) n -> p j n", p=P)
+            nc.sync.dma_start(out=dst, in_=out[:])
+
+        def empty_values(h, e, i, out, on_scalar):
             copy = nc.scalar.copy if on_scalar else nc.vector.tensor_copy
-            copy(out=out[:], in_=acc["v", h, e, i][:])
+            copy(out=out, in_=acc["v", h, e, i][:])
+
+        def store_values(h, e, i, count, out):
             row = h * N + i * P
-            nc.sync.dma_start(out=values[row:row + P, e * N:(e + 1) * N], in_=out[:])
+            dst = values[row:row + count * P, e * N:(e + 1) * N].rearrange("(i p) n -> p i n", p=P)
+            nc.sync.dma_start(out=dst, in_=out[:])
+
+        def keys_jobs(h, j0, banks, engines):
+            out = new_result(len(banks))
+            for n, b in enumerate(banks):
+                for c in range(L_PASSES):
+                    keys_pass(h, j0 + n, c, b)
+                empty_keys(h, j0 + n, out[:, n, :], engines[n])
+            store_keys(h, j0, len(banks), out)
+
+        def values_jobs(h, e, i0, banks, engines):
+            out = new_result(len(banks))
+            for n, b in enumerate(banks):
+                for c in range(L_PASSES):
+                    values_pass(h, e, i0 + n, c, b)
+                empty_values(h, e, i0 + n, out[:, n, :], engines[n])
+            store_values(h, e, i0, len(banks), out)
+
+        def down_group(h, c, t, b):
+            for g in range(D_PASSES):
+                down_pass(h, c, t, g, b)
 
         S, V = nc.scalar.copy, nc.vector.tensor_copy
 
@@ -216,138 +260,142 @@ def tile_latent_key_value_cache_s9_kernel(tc, x, down_words, down_scales, gain, 
 
 
         A, B = [0, 1, 2, 3], [4, 5, 6, 7]
+        SS, SV = (True, True), (True, False)
 
-        def keys_job(h, j, b, on_scalar):
-            for c in range(L_PASSES):
-                keys_pass(h, j, c, b)
-            finish_keys(h, j, on_scalar)
+        def q5(h, c):
+            quantise(("c", h, c), E5M2)
 
-        def values_job(h, e, i, b, on_scalar):
-            for c in range(L_PASSES):
-                values_pass(h, e, i, c, b)
-            finish_values(h, e, i, on_scalar)
+        def mix(h, c):
+            interleave(("c", h, c), latent[h, c][:], V)
 
-        def down_group(h, c, t, b):
-            for g in range(D_PASSES):
-                down_pass(h, c, t, g, b)
-
+        sort_x(0, 0, 0, V)
+        sort_x(0, 0, 1, V)
         transpose_x(0, 0, B[0:2])
+        sort_x(0, 1, 0, V)
+        sort_x(0, 1, 1, V)
         empty_x(0, 0, 0, S)
-        empty_x(0, 0, 1, V)
+        empty_x(0, 0, 1, S)
         transpose_x(0, 1, B[2:4])
-        empty_x(0, 1, 0, S)
+        permute_scales(0)
         q4("x", 0, 0)
+        permute_codes(0, 0, 2)
+        empty_x(0, 1, 0, S)
         empty_x(0, 1, 1, S)
-        permute_w(0)
         for t in range(4):
             down_pass(0, 0, t, 0, A[t])
-        permute_w(1)
-        transpose_x(0, 2, B[0:2])
+        widen_consts()
+        sort_x(0, 2, 0, V)
         q4("x", 0, 1)
+        sort_x(0, 2, 1, V)
+        transpose_x(0, 2, B[0:2])
         empty_x(0, 2, 0, S)
-        empty_x(0, 2, 1, V)
+        empty_x(0, 2, 1, S)
+        make_consts(B[2])
         for t in range(4):
             down_pass(0, 0, t, 1, A[t])
-        permute_w(2)
-        widen_consts()
+        permute_codes(0, 2, 4)
+        sort_x(0, 3, 0, V)
+        sort_x(0, 3, 1, V)
         transpose_x(0, 3, B[2:4])
         q4("x", 0, 2)
         empty_x(0, 3, 0, S)
-        empty_x(0, 3, 1, V)
-        make_consts(B[1])
-        permute_w(3)
+        empty_x(0, 3, 1, S)
         for t in range(4):
             down_pass(0, 0, t, 2, A[t])
+        permute_scales(1)
+        permute_codes(1, 0, 4)
         q4("x", 0, 3)
         for g in range(3):
             down_pass(0, 1, 0, g, B[0])
-        prep("wk", 0, 0)
-        prep("wk", 0, 1)
         for t in range(4):
             down_pass(0, 0, t, 3, A[t])
             empty_z(0, 0, t)
-        q4("wk", 0, 0)
-        q4("wk", 0, 1)
-        down_pass(0, 1, 0, 3, B[0])
-        empty_z(0, 1, 0)
+        prep("wk", 0, 0)
         prep("wk", 1, 0)
+        down_pass(0, 1, 0, 3, B[0])
         down_group(0, 1, 1, B[1])
-        empty_z(0, 1, 1)
-        interleave(("c", 0, 0), latent[0, 0][:], V)
-        q4("wk", 1, 0)
+        sort_x(1, 0, 0, V)
+        sort_x(1, 0, 1, V)
+        q4("wk", 0, 0)
         down_group(0, 1, 2, B[2])
-        empty_z(0, 1, 2)
-        quantise(("c", 0, 0), E5M2)
+        sort_x(1, 1, 0, V)
+        sort_x(1, 1, 1, V)
+        empty_z(0, 1, 0)
+        empty_z(0, 1, 1)
         transpose_x(1, 0, A[0:2])
-        empty_x(1, 0, 0, S)
-        empty_x(1, 0, 1, V)
         transpose_x(1, 1, A[2:4])
-        empty_x(1, 1, 0, S)
-        q4("x", 1, 0)
+        q4("wk", 1, 0)
+        mix(0, 0)
+        empty_x(1, 0, 0, S)
+        empty_x(1, 0, 1, S)
         down_group(0, 1, 3, B[3])
-        empty_x(1, 1, 1, V)
-        empty_z(0, 1, 3)
-        prep("wk", 1, 1)
-        for t in range(4):
-            down_pass(1, 0, t, 0, B[t])
-        transpose_x(1, 2, A[0:2])
+        sort_x(1, 2, 0, V)
+        sort_x(1, 2, 1, V)
+        q4("x", 1, 0)
+        empty_x(1, 1, 0, S)
+        empty_x(1, 1, 1, S)
+        empty_z(0, 1, 2)
+        sort_x(1, 3, 0, V)
+        sort_x(1, 3, 1, V)
+        transpose_x(1, 2, B[0:2])
+        transpose_x(1, 3, A[0:2])
         q4("x", 1, 1)
-        interleave(("c", 0, 1), latent[0, 1][:], V)
-        q4("wk", 1, 1)
+        empty_z(0, 1, 3)
         empty_x(1, 2, 0, S)
         empty_x(1, 2, 1, S)
-        for t in range(4):
-            down_pass(1, 0, t, 1, B[t])
-        transpose_x(1, 3, A[2:4])
+        q5(0, 0)
+        C = [A[2], A[3], B[2], B[3]]
+        F = [B[0], B[1], A[0], A[1]]
+        for g in range(2):
+            for t in range(4):
+                down_pass(1, 0, t, g, C[t])
         q4("x", 1, 2)
-        quantise(("c", 0, 1), E5M2)
         empty_x(1, 3, 0, S)
         empty_x(1, 3, 1, S)
-        prep("wv", 0, 0)
+        mix(0, 1)
+        prep("wk", 0, 1, S)
         for t in range(4):
-            down_pass(1, 0, t, 2, B[t])
+            down_pass(1, 0, t, 2, C[t])
         q4("x", 1, 3)
-        q4("wv", 0, 0)
-        keys_job(0, 0, A[0], True)
-        keys_job(0, 1, A[1], True)
-        prep("wv", 1, 0)
-        prep("wv", 0, 1)
+        q5(0, 1)
+        prep("wk", 1, 1)
         for t in range(4):
-            down_pass(1, 0, t, 3, B[t])
+            down_pass(1, 0, t, 3, C[t])
             empty_z(1, 0, t)
+        q4("wk", 0, 1)
+        q4("wk", 1, 1)
+        keys_jobs(0, 0, F[0:2], SS)
+        keys_jobs(0, 2, F[2:4], SS)
+        prep("wv", 0, 0)
+        mix(1, 0)
+        q4("wv", 0, 0)
+        prep("wv", 1, 0)
+        q5(1, 0)
+        for t in range(4):
+            down_group(1, 1, t, C[t])
+            empty_z(1, 1, t)
         q4("wv", 1, 0)
-        q4("wv", 0, 1)
-        down_group(1, 1, 0, A[2])
-        keys_job(0, 2, A[3], True)
-        keys_job(0, 3, A[0], True)
-        prep("wv", 1, 1)
-        interleave(("c", 1, 0), latent[1, 0][:], V)
-        down_group(1, 1, 1, A[1])
-        empty_z(1, 1, 0)
-        keys_job(0, 4, B[0], True)
-        empty_z(1, 1, 1)
-        keys_job(0, 5, B[1], True)
-        q4("wv", 1, 1)
-        quantise(("c", 1, 0), E5M2)
-        down_group(1, 1, 2, B[2])
-        prep("wv", 0, 2)
-        prep("wv", 1, 2)
-        empty_z(1, 1, 2)
-        keys_job(0, 6, B[3], True)
-        keys_job(0, 7, A[2], True)
-        q4("wv", 0, 2)
-        q4("wv", 1, 2)
-        down_group(1, 1, 3, A[3])
-        empty_z(1, 1, 3)
-        ring = [A[0], A[1], B[0], B[1], B[2], B[3], A[2], A[3]]
-        jobs = [("v", 0, e, i) for e in range(3) for i in range(4)] + [("k", 1, j) for j in range(8)] + [("v", 1, e, i) for e in range(3) for i in range(4)]
+        mix(1, 1)
+        prep("wv", 0, 1)
+        q5(1, 1)
+        ring = F + C
+        jobs = ([("k", 0, j) for j in (4, 6)] + [("v", 0, 0, 0), ("v", 0, 0, 2)] + [("k", 1, j) for j in (0, 2, 4, 6)] + [("v", 1, 0, 0), ("v", 1, 0, 2)]
+                + [("v", h, e, i) for e in (1, 2) for h in range(2) for i in (0, 2)])
+        side = {
+            0: [lambda: prep("wv", 1, 1), lambda: q4("wv", 0, 1)],
+            2: [lambda: prep("wv", 0, 2), lambda: q4("wv", 1, 1)],
+            4: [lambda: prep("wv", 1, 2), lambda: q4("wv", 0, 2)],
+            6: [lambda: q4("wv", 1, 2)],
+        }
         for step, job in enumerate(jobs):
-            if step == 2:
-                interleave(("c", 1, 1), latent[1, 1][:], V)
-            if step == 6:
-                quantise(("c", 1, 1), E5M2)
-            on_scalar = step % 2 == 0 or step == 3
+            for f in side.get(step, []):
+                f()
+            banks = [ring[(2 * step) % 8], ring[(2 * step + 1) % 8]]
+            engines = SV if step >= 9 else SS
             if job[0] == "k":
-                keys_job(job[1], job[2], ring[step % 8], on_scalar)
+                keys_jobs(job[1], job[2], banks, engines)
+            elif step < len(jobs) - 1:
+                values_jobs(job[1], job[2], job[3], banks, engines)
             else:
-                values_job(job[1], job[2], job[3], ring[step % 8], on_scalar)
+                values_jobs(job[1], job[2], job[3], banks[0:1], engines[0:1])
+                values_jobs(job[1], job[2], job[3] + 1, banks[1:2], engines[1:2])

@@ -15,27 +15,32 @@ E4M3 = mybir.dt.float8_e4m3fn_x4
 E5M2 = mybir.dt.float8_e5m2_x4
 E2M1 = mybir.dt.float4_e2m1fn_x4
 IDENTITY = mybir.ActivationFunctionType.Identity
-MULT = mybir.AluOpType.mult
 ADD = mybir.AluOpType.add
 
 P = 128
 PACK = 4
 KP = P * PACK
 N = 512
-HALVES = T // N
 D_PASSES = D // KP
 L_PASSES = L // KP
 TILES = N // P
+PAIRS = TILES // 2
 RUN = 4
+SCALE_PASSES = 2
+SORTED_BUFS = 4
+GROUPED_BUFS = 5
+RESULT_BUFS = 7
+BIAS_ROW = 32
 
 
 def tile_latent_key_value_cache_s9_kernel(tc, x, down_words, down_scales, gain, shift, wk, bk, wv, keys, values):
     nc = tc.nc
     with ExitStack() as ctx:
         keep = ctx.enter_context(tc.tile_pool(name="keep", bufs=1))
-        stage = ctx.enter_context(tc.tile_pool(name="stage", bufs=4))
+        stage = ctx.enter_context(tc.tile_pool(name="stage", bufs=2))
         psum = ctx.enter_context(tc.psum_pool(name="psum", bufs=1))
         ctx.enter_context(tc.manual_schedule())
+        scalar_copy, vector_copy = nc.scalar.copy, nc.vector.tensor_copy
 
         def kept(name, shape, dtype):
             return keep.tile(shape, dtype, name=name, align_bytes=64)
@@ -43,127 +48,158 @@ def tile_latent_key_value_cache_s9_kernel(tc, x, down_words, down_scales, gain, 
         def bank(b, shape):
             return psum.tile(shape, F32, name="bank%d" % b)
 
+        def grouped_tile():
+            return stage.tile([P, PACK * N], BF16, name="grouped", bufs=GROUPED_BUFS, align_bytes=64)
+
+        def result_tile(shape, dtype):
+            return stage.tile(shape, dtype, name="result", bufs=RESULT_BUFS)
+
         ident = kept("ident", [P, P], F32)
         make_identity(nc, ident[:])
+
         scale_raw = {}
-        for c in range(L_PASSES):
-            scale_raw[c] = kept("scale_raw%d" % c, [P, D_PASSES * KP // 4], I32)
-            nc.vector.memset(scale_raw[c][:], 0)
+        for g0 in range(0, D_PASSES, SCALE_PASSES):
+            scale_raw[g0] = kept("scale_raw%d" % g0, [P, SCALE_PASSES * L // 4], I32)
+            nc.vector.memset(scale_raw[g0][:], 0)
+        zero = kept("zero", [P, 1], F32)
+        nc.vector.memset(zero[:], 0.0)
         rows32 = kept("rows32", [P, N], F32)
-        nc.vector.memset(rows32[:], 0.0)
-        warm = kept("warm", [P, 1], F32)
-        nc.scalar.activation(out=warm[:], in_=rows32[:, 0:1], func=IDENTITY)
+        nc.scalar.activation(out=rows32[:], in_=zero[:].to_broadcast([P, N]), func=IDENTITY)
 
-        x_raw, w_raw, wk_raw, wv_raw = {}, {}, {}, {}
+        x_raw, w_raw, weight_raw = {}, {}, {}
 
-        def load_x(h, g, pairs=(0, 1)):
-            raw = kept("x_raw%d%d%d" % (h, g, pairs[0]), [P, 2 * len(pairs), KP], BF16)
+        def load_x(h, g0, g1, pairs):
+            raw = kept("x_raw%d%d%d" % (h, g0, pairs[0]), [P, 2 * len(pairs), (g1 - g0) * KP], BF16)
             row = h * N + pairs[0] * 2 * P
-            src = x[row:row + len(pairs) * 2 * P, g * KP:(g + 1) * KP].rearrange("(i p) k -> p i k", p=P)
+            src = x[row:row + len(pairs) * 2 * P, g0 * KP:g1 * KP].rearrange("(i p) k -> p i k", p=P)
             nc.sync.dma_start(out=raw[:], in_=src)
-            for n, pair in enumerate(pairs):
-                x_raw[h, g, pair] = raw[:, 2 * n:2 * n + 2, :]
+            for g in range(g0, g1):
+                x_raw[h, g, pairs] = raw[:, :, (g - g0) * KP:(g - g0 + 1) * KP]
 
-        def load_w(c, g0, g1):
-            w_raw[c, g0] = kept("w_raw%d%d" % (c, g0), [P, g1 - g0, KP // 2], I32)
-            src = down_words[g0:g1, :, 2 * c * KP:2 * (c + 1) * KP].bitcast(I32).rearrange("g p n -> p g n")
-            nc.sync.dma_start(out=w_raw[c, g0][:], in_=src)
+        def load_w(g):
+            w_raw[g] = result_tile([P, KP], I32)
+            nc.sync.dma_start(out=w_raw[g][:], in_=down_words[g].bitcast(I32))
 
-        def load_w_scales(c):
+        def load_w_scales(g0):
             for r in range(4):
                 nc.sync.dma_start(
-                    out=scale_raw[c][r:P:32, :].rearrange("q (g n) -> q g n", g=D_PASSES),
-                    in_=down_scales[:, r:16:4, c * KP:(c + 1) * KP].bitcast(I32).rearrange("g q n -> q g n"))
+                    out=scale_raw[g0][r:P:32, :].rearrange("q (g n) -> q g n", g=SCALE_PASSES),
+                    in_=down_scales[g0:g0 + SCALE_PASSES, r:16:4, :].bitcast(I32).rearrange("g q n -> q g n"))
 
-        def load_second_weight(raw, name, weight, c):
-            raw[c] = kept("%s%d" % (name, c), [P, PACK, weight.shape[1]], BF16)
-            rows = weight[c * KP:(c + 1) * KP, :].rearrange("(m t b) n -> b m t n", t=PACK, b=RUN)
-            for b in range(RUN):
-                nc.sync.dma_start(out=raw[c][b:P:RUN, :, :], in_=rows[b])
-
-        load_x(0, 0, (0,))
-        load_x(0, 0, (1,))
-        load_x(0, 1)
-        load_w_scales(0)
-        load_w(0, 0, 2)
-        load_x(0, 2)
         rows16 = kept("rows16", [P, N], BF16)
-        nc.sync.dma_start(out=rows16[0:2, :], in_=gain.rearrange("(c n) -> c n", n=N))
-        nc.sync.dma_start(out=rows16[2:4, :], in_=shift.rearrange("(c n) -> c n", n=N))
-        nc.sync.dma_start(out=rows16[32:34, :], in_=bk.rearrange("(c n) -> c n", n=N))
-        load_w(0, 2, 4)
-        load_x(0, 3)
-        load_w_scales(1)
-        load_w(1, 0, 4)
-        load_second_weight(wk_raw, "wk_raw", wk, 0)
-        load_second_weight(wk_raw, "wk_raw", wk, 1)
-        for g in range(D_PASSES):
-            load_x(1, g)
-        load_second_weight(wv_raw, "wv_raw", wv, 0)
-        load_second_weight(wv_raw, "wv_raw", wv, 1)
+
+        def load_channel_vectors():
+            nc.sync.dma_start(out=rows16[0:2, :], in_=gain.rearrange("(c n) -> c n", n=N))
+            nc.sync.dma_start(out=rows16[2:4, :], in_=shift.rearrange("(c n) -> c n", n=N))
+            nc.sync.dma_start(out=rows16[BIAS_ROW:BIAS_ROW + 2, :], in_=bk.rearrange("(c n) -> c n", n=N))
+
+        def load_weight(kind, c, e0, e1):
+            weight = wk if kind == "wk" else wv
+            raw = kept("%s_raw%d%d" % (kind, c, e0), [P, PACK, (e1 - e0) * N], BF16)
+            rows = weight[c * KP:(c + 1) * KP, e0 * N:e1 * N].rearrange("(m t b) n -> b m t n", t=PACK, b=RUN)
+            for b in range(RUN):
+                nc.sync.dma_start(out=raw[b:P:RUN, :, :], in_=rows[b])
+            for e in range(e0, e1):
+                weight_raw[kind, c, e] = raw[:, :, (e - e0) * N:(e - e0 + 1) * N]
+
+        both = tuple(range(PAIRS))
+        load_x(0, 0, 1, (0,))
+        load_x(0, 0, 1, (1,))
+        load_x(0, 1, 2, both)
+        load_w(0)
+        load_w_scales(0)
+        load_x(0, 2, 3, both)
+        load_w(1)
+        load_channel_vectors()
+        load_x(0, 3, 4, both)
+        load_w_scales(2)
+        load_w(2)
+        load_w(3)
+        load_weight("wv", 0, 0, 2)
+        load_x(1, 0, 2, both)
+        load_x(1, 2, 4, both)
+        load_weight("wv", 1, 0, 2)
+        for c in range(L_PASSES):
+            load_weight("wv", c, 2, 3)
+        for c in range(L_PASSES):
+            load_weight("wk", c, 0, 2)
 
         w_codes, w_scales = {}, {}
 
-        def permute_scales(c):
-            w_scales[c] = kept("w_scales%d" % c, [P, D_PASSES * KP], U8)
+        def reorder_w_scales(g0):
+            planes = kept("w_scales%d" % g0, [P, SCALE_PASSES * L], U8)
             nc.vector.tensor_copy(
-                out=w_scales[c][:].bitcast(I32).rearrange("p (g t a m) -> p g a t m", g=D_PASSES, t=PACK, m=4),
-                in_=scale_raw[c][:].rearrange("p (g a m t) -> p g a t m", g=D_PASSES, t=PACK, m=4))
+                out=planes[:].bitcast(I32).rearrange("p (j t a i) -> p j a t i", j=SCALE_PASSES * L_PASSES, t=PACK, i=4),
+                in_=scale_raw[g0][:].rearrange("p (j a i t) -> p j a t i", j=SCALE_PASSES * L_PASSES, t=PACK, i=4))
+            for g in range(g0, g0 + SCALE_PASSES):
+                for c in range(L_PASSES):
+                    first = (g - g0) * L + c * KP
+                    w_scales[c, g] = planes[:, first:first + KP]
 
-        def permute_codes(c, g0, g1):
-            codes = kept("w_codes%d%d" % (c, g0), [P, (g1 - g0) * 2 * KP], U8)
+        def reorder_w_codes(g):
+            codes = kept("w_codes%d" % g, [P, 2 * L], U8)
             nc.vector.tensor_copy(
-                out=codes[:].bitcast(I32).rearrange("p (g t m w) -> p g t m w", g=g1 - g0, t=PACK, w=2),
-                in_=w_raw[c, g0][:].rearrange("p g (m t w) -> p g t m w", t=PACK, w=2))
-            for g in range(g0, g1):
-                w_codes[c, g] = codes[:, (g - g0) * 2 * KP:(g - g0 + 1) * 2 * KP]
+                out=codes[:].bitcast(I32).rearrange("p (c t m w) -> p c t m w", c=L_PASSES, t=PACK, w=2),
+                in_=w_raw[g][:].rearrange("p (c m t w) -> p c t m w", c=L_PASSES, t=PACK, w=2))
+            for c in range(L_PASSES):
+                w_codes[c, g] = codes[:, c * 2 * KP:(c + 1) * 2 * KP]
 
         sorted_x, turned, grouped, quantised = {}, {}, {}, {}
 
-        def sort_x(h, g, pair, copy):
-            sorted_x[h, g, pair] = stage.tile([P, 2, 2, P], F32, name="sorted_x", bufs=6, align_bytes=64)
-            copy(out=sorted_x[h, g, pair][:], in_=x_raw[h, g, pair].bitcast(F32).rearrange("p i (m u) -> p i u m", u=2))
+        def sort_x(h, g, pairs):
+            if pairs[0] == 0:
+                sorted_x[h, g] = stage.tile([P, TILES, 2, P], F32, name="sorted_x", bufs=SORTED_BUFS, align_bytes=64)
+            vector_copy(out=sorted_x[h, g][:, 2 * pairs[0]:2 * pairs[-1] + 2, :, :],
+                        in_=x_raw[h, g, pairs].bitcast(F32).rearrange("p i (m u) -> p i u m", u=2))
+
+        def transpose_pair(h, g, pair, b):
+            turned[h, g, pair] = bank(b, [P, 2, 2, P])
+            for i in range(2):
+                for u in range(2):
+                    nc.tensor.transpose(turned[h, g, pair][:, i, u, :], sorted_x[h, g][:, 2 * pair + i, u, :], ident[:])
 
         def transpose_x(h, g, banks):
-            for pair in range(2):
-                turned[h, g, pair] = bank(banks[pair], [P, 2, 2, P])
-                for i in range(2):
-                    for u in range(2):
-                        nc.tensor.transpose(turned[h, g, pair][:, i, u, :], sorted_x[h, g, pair][:, i, u, :], ident[:])
+            for pair in range(PAIRS):
+                transpose_pair(h, g, pair, banks[pair])
 
-        def new_grouped(key):
-            grouped[key] = stage.tile([P, PACK * N], BF16, name="grouped", align_bytes=64)
-
-        def empty_x(h, g, pair, copy):
-            if pair == 0:
-                new_grouped(("x", h, g))
-            dst = grouped["x", h, g][:, pair * 2 * N:(pair + 1) * 2 * N].bitcast(F32)
-            copy(out=dst.rearrange("p (i r u) -> p i r u", i=2, u=2), in_=turned[h, g, pair][:].rearrange("p i u r -> p i r u"))
+        def empty_x(h, g, copy):
+            grouped["x", h, g] = grouped_tile()
+            for pair in range(PAIRS):
+                dst = grouped["x", h, g][:, pair * 2 * N:(pair + 1) * 2 * N].bitcast(F32)
+                copy(out=dst.rearrange("p (i r u) -> p i r u", i=2, u=2),
+                     in_=turned[h, g, pair][:].rearrange("p i u r -> p i r u"))
 
         def interleave(key, src, copy):
-            new_grouped(key)
+            grouped[key] = grouped_tile()
             copy(out=grouped[key][:].rearrange("p (c i t) -> p c t i", t=PACK, i=4),
                  in_=src.rearrange("p t (c i) -> p c t i", i=4))
 
-        def quantise(key, fmt):
-            name = "_".join(str(k) for k in key)
-            codes = kept("codes_" + name, [P, N], U32)
-            scales = kept("scales_" + name, [P, N], U8)
-            nc.vector.quantize_mx(out=codes[:].bitcast(fmt), scales=scales[:], in_=grouped[key][:])
+        def quantise(key, pieces=1):
+            name = "%s_%d_%d" % key
+            codes, scales = kept("codes_" + name, [P, N], U32), kept("scales_" + name, [P, N], U8)
+            fmt = E5M2 if key[0] == "c" else E4M3
+            width = N // pieces
+            for n in range(pieces):
+                cols = slice(n * width, (n + 1) * width)
+                nc.vector.quantize_mx(out=codes[:, cols].bitcast(fmt), scales=scales[:, cols],
+                                      in_=grouped[key][:, PACK * n * width:PACK * (n + 1) * width])
             quantised[key] = (codes, scales)
 
-        consts = kept("consts", [P, PACK, 64], F32)
+        def interleave_weight(kind, c, e):
+            interleave((kind, c, e), weight_raw[kind, c, e], vector_copy)
 
-        def widen_consts():
-            nc.scalar.copy(out=rows32[0:4, :].rearrange("p (t m b) -> p t m b", t=PACK, b=RUN),
-                                  in_=rows16[0:4, :].rearrange("p (m t b) -> p t m b", t=PACK, b=RUN))
-            nc.scalar.copy(out=rows32[32:34, :], in_=rows16[32:34, :])
+        consts = kept("consts", [P, PACK, 2 * BIAS_ROW], F32)
 
-        def make_consts(b):
+        def widen_channel_vectors():
+            scalar_copy(out=rows32[0:4, :].rearrange("p (t m b) -> p t m b", t=PACK, b=RUN),
+                        in_=rows16[0:4, :].rearrange("p (m t b) -> p t m b", t=PACK, b=RUN))
+            scalar_copy(out=rows32[BIAS_ROW:BIAS_ROW + 2, :], in_=rows16[BIAS_ROW:BIAS_ROW + 2, :])
+
+        def transpose_channel_vectors(b):
             cols = bank(b, [P, PACK, P])
             for t in range(PACK):
                 nc.tensor.transpose(cols[:, t, :], rows32[:, t * P:(t + 1) * P], ident[:])
-            nc.scalar.copy(out=consts[:], in_=cols[:, :, 0:64])
+            scalar_copy(out=consts[:], in_=cols[:, :, 0:2 * BIAS_ROW])
 
         z, latent = {}, {}
 
@@ -174,228 +210,174 @@ def tile_latent_key_value_cache_s9_kernel(tc, x, down_words, down_scales, gain, 
             nc.tensor.matmul_mx(
                 out=z[h, c, t][:],
                 lhsT=w_codes[c, g][:, 2 * t * P:2 * (t + 1) * P].bitcast(E2M1),
-                lhsT_scale=w_scales[c][:, g * KP + t * P:g * KP + (t + 1) * P],
+                lhsT_scale=w_scales[c, g][:, t * P:(t + 1) * P],
                 rhs=codes[:].bitcast(E4M3), rhs_scale=scales[:], start=(g == 0), stop=(g == D_PASSES - 1))
-
-        def empty_z(h, c, t, on_scalar=True):
-            if t == 0:
-                latent[h, c] = stage.tile([P, PACK, N], BF16, name="latent", bufs=2, align_bytes=64)
-            g_col, s_col = consts[:, t, c:c + 1], consts[:, t, 2 + c:3 + c]
-            if on_scalar:
-                nc.scalar.activation(out=latent[h, c][:, t, :], in_=z[h, c, t][:], func=IDENTITY, scale=g_col, bias=s_col)
-            else:
-                nc.vector.tensor_scalar(out=latent[h, c][:, t, :], in0=z[h, c, t][:], scalar1=g_col, scalar2=s_col, op0=MULT, op1=ADD)
-
-        acc = {}
-
-        def keys_pass(h, j, c, b):
-            if c == 0:
-                acc["k", h, j] = bank(b, [P, N])
-            wc, ws = quantised["wk", c, j // TILES]
-            cc, cs = quantised["c", h, c]
-            cols = slice((j % TILES) * P, (j % TILES + 1) * P)
-            nc.tensor.matmul_mx(out=acc["k", h, j][:], lhsT=wc[:, cols].bitcast(E4M3), lhsT_scale=ws[:, cols],
-                                rhs=cc[:].bitcast(E5M2), rhs_scale=cs[:], start=(c == 0), stop=(c == L_PASSES - 1))
-
-        def values_pass(h, e, i, c, b):
-            if c == 0:
-                acc["v", h, e, i] = bank(b, [P, N])
-            wc, ws = quantised["wv", c, e]
-            cc, cs = quantised["c", h, c]
-            cols = slice(i * P, (i + 1) * P)
-            nc.tensor.matmul_mx(out=acc["v", h, e, i][:], lhsT=cc[:, cols].bitcast(E5M2), lhsT_scale=cs[:, cols],
-                                rhs=wc[:].bitcast(E4M3), rhs_scale=ws[:], start=(c == 0), stop=(c == L_PASSES - 1))
-
-        def new_result(count):
-            return stage.tile([P, count, N], F32, name="result", bufs=7)
-
-        def empty_keys(h, j, out, on_scalar):
-            bias = consts[:, j % PACK, 32 + j // PACK:33 + j // PACK]
-            if on_scalar:
-                nc.scalar.activation(out=out, in_=acc["k", h, j][:], func=IDENTITY, bias=bias)
-            else:
-                nc.vector.tensor_scalar(out=out, in0=acc["k", h, j][:], scalar1=bias, scalar2=None, op0=ADD)
-
-        def store_keys(h, j, count, out):
-            dst = keys[j * P:(j + count) * P, h * N:(h + 1) * N].rearrange("(j p) n -> p j n", p=P)
-            nc.sync.dma_start(out=dst, in_=out[:])
-
-        def empty_values(h, e, i, out, on_scalar):
-            copy = nc.scalar.copy if on_scalar else nc.vector.tensor_copy
-            copy(out=out, in_=acc["v", h, e, i][:])
-
-        def store_values(h, e, i, count, out):
-            row = h * N + i * P
-            dst = values[row:row + count * P, e * N:(e + 1) * N].rearrange("(i p) n -> p i n", p=P)
-            nc.sync.dma_start(out=dst, in_=out[:])
-
-        def keys_jobs(h, j0, banks, engines):
-            out = new_result(len(banks))
-            for n, b in enumerate(banks):
-                for c in range(L_PASSES):
-                    keys_pass(h, j0 + n, c, b)
-                empty_keys(h, j0 + n, out[:, n, :], engines[n])
-            store_keys(h, j0, len(banks), out)
-
-        def values_jobs(h, e, i0, banks, engines):
-            out = new_result(len(banks))
-            for n, b in enumerate(banks):
-                for c in range(L_PASSES):
-                    values_pass(h, e, i0 + n, c, b)
-                empty_values(h, e, i0 + n, out[:, n, :], engines[n])
-            store_values(h, e, i0, len(banks), out)
 
         def down_group(h, c, t, b):
             for g in range(D_PASSES):
                 down_pass(h, c, t, g, b)
 
-        S, V = nc.scalar.copy, nc.vector.tensor_copy
+        def empty_z(h, c, t):
+            if t == 0:
+                latent[h, c] = stage.tile([P, PACK, N], BF16, name="latent", align_bytes=64)
+            nc.scalar.activation(out=latent[h, c][:, t, :], in_=z[h, c, t][:], func=IDENTITY,
+                                 scale=consts[:, t, c:c + 1], bias=consts[:, t, 2 + c:3 + c])
 
-        def prep(kind, c, chunk, copy=V):
-            raw = wk_raw if kind == "wk" else wv_raw
-            interleave((kind, c, chunk), raw[c][:, :, chunk * N:(chunk + 1) * N], copy)
+        def interleave_latent(h, c, copy):
+            interleave(("c", h, c), latent[h, c][:], copy)
 
-        def q4(*key):
-            quantise(key, E4M3)
+        def second_stage_group(b, fixed, fixed_fmt, cols, moving, moving_fmt):
+            acc = bank(b, [P, N])
+            for c in range(L_PASSES):
+                (fixed_codes, fixed_scales), (moving_codes, moving_scales) = quantised[fixed(c)], quantised[moving(c)]
+                nc.tensor.matmul_mx(out=acc[:], lhsT=fixed_codes[:, cols].bitcast(fixed_fmt), lhsT_scale=fixed_scales[:, cols],
+                                    rhs=moving_codes[:].bitcast(moving_fmt), rhs_scale=moving_scales[:],
+                                    start=(c == 0), stop=(c == L_PASSES - 1))
+            return acc
 
+        def values_block(h, i, e, b, out, copy):
+            acc = second_stage_group(b, lambda c: ("c", h, c), E5M2, slice(i * P, (i + 1) * P), lambda c: ("wv", c, e), E4M3)
+            copy(out=out, in_=acc[:])
 
-        A, B = [0, 1, 2, 3], [4, 5, 6, 7]
-        SS, SV = (True, True), (True, False)
+        def keys_block(j, h, b, out):
+            cols = slice((j % TILES) * P, (j % TILES + 1) * P)
+            acc = second_stage_group(b, lambda c: ("wk", c, j // TILES), E4M3, cols, lambda c: ("c", h, c), E5M2)
+            bias = consts[:, j % PACK, BIAS_ROW + j // PACK:BIAS_ROW + j // PACK + 1]
+            if h == 0:
+                nc.vector.tensor_scalar(out=out, in0=acc[:], scalar1=bias, scalar2=None, op0=ADD)
+            else:
+                nc.scalar.activation(out=out, in_=acc[:], func=IDENTITY, bias=bias)
 
-        def q5(h, c):
-            quantise(("c", h, c), E5M2)
+        def values_pair(h, pair, e, banks):
+            out = result_tile([P, 2, N], F32)
+            for n in range(2):
+                values_block(h, 2 * pair + n, e, banks[n], out[:, n, :], scalar_copy)
+            row = h * N + 2 * pair * P
+            nc.sync.dma_start(out=values[row:row + 2 * P, e * N:(e + 1) * N].rearrange("(i p) n -> p i n", p=P), in_=out[:])
 
-        def mix(h, c):
-            interleave(("c", h, c), latent[h, c][:], V)
+        def values_rows(h, i, banks):
+            out = result_tile([P, E], F32)
+            for e in range(E // N):
+                values_block(h, i, e, banks[e], out[:, e * N:(e + 1) * N], vector_copy if e == 0 else scalar_copy)
+            row = h * N + i * P
+            nc.sync.dma_start(out=values[row:row + P, :], in_=out[:])
 
-        sort_x(0, 0, 0, V)
-        sort_x(0, 0, 1, V)
-        transpose_x(0, 0, B[0:2])
-        sort_x(0, 1, 0, V)
-        sort_x(0, 1, 1, V)
-        empty_x(0, 0, 0, S)
-        empty_x(0, 0, 1, S)
-        transpose_x(0, 1, B[2:4])
-        permute_scales(0)
-        q4("x", 0, 0)
-        permute_codes(0, 0, 2)
-        empty_x(0, 1, 0, S)
-        empty_x(0, 1, 1, S)
-        for t in range(4):
-            down_pass(0, 0, t, 0, A[t])
-        widen_consts()
-        sort_x(0, 2, 0, V)
-        q4("x", 0, 1)
-        sort_x(0, 2, 1, V)
-        transpose_x(0, 2, B[0:2])
-        empty_x(0, 2, 0, S)
-        empty_x(0, 2, 1, S)
-        make_consts(B[2])
-        for t in range(4):
-            down_pass(0, 0, t, 1, A[t])
-        permute_codes(0, 2, 4)
-        sort_x(0, 3, 0, V)
-        sort_x(0, 3, 1, V)
-        transpose_x(0, 3, B[2:4])
-        q4("x", 0, 2)
-        empty_x(0, 3, 0, S)
-        empty_x(0, 3, 1, S)
-        for t in range(4):
-            down_pass(0, 0, t, 2, A[t])
-        permute_scales(1)
-        permute_codes(1, 0, 4)
-        q4("x", 0, 3)
-        for g in range(3):
-            down_pass(0, 1, 0, g, B[0])
-        for t in range(4):
-            down_pass(0, 0, t, 3, A[t])
+        def keys_rows(j, banks):
+            out = result_tile([P, T], F32)
+            for h in range(2):
+                keys_block(j, h, banks[h], out[:, h * N:(h + 1) * N])
+            nc.sync.dma_start(out=keys[j * P:(j + 1) * P, :], in_=out[:])
+
+        def keys_half_rows(j, h, b):
+            out = result_tile([P, N], F32)
+            keys_block(j, h, b, out[:])
+            nc.sync.dma_start(out=keys[j * P:(j + 1) * P, h * N:(h + 1) * N], in_=out[:])
+
+        sums, spare = [0, 1, 2, 3, 4, 5], [6, 7]
+        for pair in range(PAIRS):
+            sort_x(0, 0, (pair,))
+            transpose_pair(0, 0, pair, spare[pair])
+        empty_x(0, 0, scalar_copy)
+        sort_x(0, 1, both)
+        transpose_x(0, 1, sums[4:6])
+        empty_x(0, 1, scalar_copy)
+        for g in range(D_PASSES):
+            if g == D_PASSES - 1:
+                reorder_w_codes(g)
+                transpose_channel_vectors(spare[0])
+            quantise(("x", 0, g), PAIRS)
+            if g % SCALE_PASSES == 0:
+                reorder_w_scales(g)
+            if g < D_PASSES - 1:
+                reorder_w_codes(g)
+            for n, b in enumerate(sums):
+                down_pass(0, n // PACK, n % PACK, g, b)
+            if g + 2 < D_PASSES:
+                sort_x(0, g + 2, both)
+                transpose_x(0, g + 2, spare)
+                if g + 2 == D_PASSES - 1:
+                    widen_channel_vectors()
+                empty_x(0, g + 2, scalar_copy)
+
+        for t in range(PACK):
             empty_z(0, 0, t)
-        prep("wk", 0, 0)
-        prep("wk", 1, 0)
-        down_pass(0, 1, 0, 3, B[0])
-        down_group(0, 1, 1, B[1])
-        sort_x(1, 0, 0, V)
-        sort_x(1, 0, 1, V)
-        q4("wk", 0, 0)
-        down_group(0, 1, 2, B[2])
-        sort_x(1, 1, 0, V)
-        sort_x(1, 1, 1, V)
+        interleave_weight("wv", 0, 0)
+        interleave_weight("wv", 0, 1)
+        sort_x(1, 0, both)
+        sort_x(1, 1, both)
+        quantise(("wv", 0, 0))
+        down_group(0, 1, 2, spare[1])
         empty_z(0, 1, 0)
         empty_z(0, 1, 1)
-        transpose_x(1, 0, A[0:2])
-        transpose_x(1, 1, A[2:4])
-        q4("wk", 1, 0)
-        mix(0, 0)
-        empty_x(1, 0, 0, S)
-        empty_x(1, 0, 1, S)
-        down_group(0, 1, 3, B[3])
-        sort_x(1, 2, 0, V)
-        sort_x(1, 2, 1, V)
-        q4("x", 1, 0)
-        empty_x(1, 1, 0, S)
-        empty_x(1, 1, 1, S)
+        transpose_x(1, 0, sums[0:2])
+        transpose_x(1, 1, sums[2:4])
+        empty_x(1, 0, vector_copy)
+        empty_x(1, 1, scalar_copy)
+        sort_x(1, 2, both)
+        sort_x(1, 3, both)
+        down_group(0, 1, 3, spare[0])
         empty_z(0, 1, 2)
-        sort_x(1, 3, 0, V)
-        sort_x(1, 3, 1, V)
-        transpose_x(1, 2, B[0:2])
-        transpose_x(1, 3, A[0:2])
-        q4("x", 1, 1)
+        transpose_x(1, 2, sums[4:6])
+        transpose_x(1, 3, [spare[1], sums[0]])
         empty_z(0, 1, 3)
-        empty_x(1, 2, 0, S)
-        empty_x(1, 2, 1, S)
-        q5(0, 0)
-        C = [A[2], A[3], B[2], B[3]]
-        F = [B[0], B[1], A[0], A[1]]
-        for g in range(2):
-            for t in range(4):
-                down_pass(1, 0, t, g, C[t])
-        q4("x", 1, 2)
-        empty_x(1, 3, 0, S)
-        empty_x(1, 3, 1, S)
-        mix(0, 1)
-        prep("wk", 0, 1, S)
-        for t in range(4):
-            down_pass(1, 0, t, 2, C[t])
-        q4("x", 1, 3)
-        q5(0, 1)
-        prep("wk", 1, 1)
-        for t in range(4):
-            down_pass(1, 0, t, 3, C[t])
+        quantise(("x", 1, 0))
+        quantise(("x", 1, 1))
+        quantise(("wv", 0, 1))
+        empty_x(1, 2, scalar_copy)
+        empty_x(1, 3, scalar_copy)
+        quantise(("x", 1, 2))
+        interleave_latent(0, 0, vector_copy)
+        quantise(("x", 1, 3))
+        interleave_latent(0, 1, scalar_copy)
+
+        ring = [sums[1], sums[2], sums[3], spare[0], sums[4], sums[5], spare[1], sums[0]]
+        for g in range(D_PASSES):
+            for t in range(PACK):
+                down_pass(1, 0, t, g, ring[t])
+        for t in range(PACK):
             empty_z(1, 0, t)
-        q4("wk", 0, 1)
-        q4("wk", 1, 1)
-        keys_jobs(0, 0, F[0:2], SS)
-        keys_jobs(0, 2, F[2:4], SS)
-        prep("wv", 0, 0)
-        mix(1, 0)
-        q4("wv", 0, 0)
-        prep("wv", 1, 0)
-        q5(1, 0)
-        for t in range(4):
-            down_group(1, 1, t, C[t])
+        quantise(("c", 0, 0))
+        interleave_weight("wv", 1, 0)
+        quantise(("c", 0, 1))
+        quantise(("wv", 1, 0))
+        interleave_weight("wv", 1, 1)
+        interleave_weight("wv", 0, 2)
+        quantise(("wv", 1, 1))
+        interleave_weight("wv", 1, 2)
+        quantise(("wv", 0, 2))
+        quantise(("wv", 1, 2))
+        interleave_latent(1, 0, vector_copy)
+
+        free = ring[PACK:] + ring[:PACK]
+
+        def take(count):
+            taken = free[:count]
+            free[:] = free[count:] + taken
+            return taken
+
+        for t in range(PACK):
+            down_group(1, 1, t, take(1)[0])
             empty_z(1, 1, t)
-        q4("wv", 1, 0)
-        mix(1, 1)
-        prep("wv", 0, 1)
-        q5(1, 1)
-        ring = F + C
-        jobs = ([("k", 0, j) for j in (4, 6)] + [("v", 0, 0, 0), ("v", 0, 0, 2)] + [("k", 1, j) for j in (0, 2, 4, 6)] + [("v", 1, 0, 0), ("v", 1, 0, 2)]
-                + [("v", h, e, i) for e in (1, 2) for h in range(2) for i in (0, 2)])
-        side = {
-            0: [lambda: prep("wv", 1, 1), lambda: q4("wv", 0, 1)],
-            2: [lambda: prep("wv", 0, 2), lambda: q4("wv", 1, 1)],
-            4: [lambda: prep("wv", 1, 2), lambda: q4("wv", 0, 2)],
-            6: [lambda: q4("wv", 1, 2)],
-        }
-        for step, job in enumerate(jobs):
-            for f in side.get(step, []):
-                f()
-            banks = [ring[(2 * step) % 8], ring[(2 * step + 1) % 8]]
-            engines = SV if step >= 9 else SS
-            if job[0] == "k":
-                keys_jobs(job[1], job[2], banks, engines)
-            elif step < len(jobs) - 1:
-                values_jobs(job[1], job[2], job[3], banks, engines)
-            else:
-                values_jobs(job[1], job[2], job[3], banks[0:1], engines[0:1])
-                values_jobs(job[1], job[2], job[3] + 1, banks[1:2], engines[1:2])
+            if t in (1, 2):
+                values_pair(0, t - 1, 0, take(2))
+        interleave_latent(1, 1, vector_copy)
+        quantise(("c", 1, 0))
+        quantise(("c", 1, 1))
+        interleave_weight("wk", 0, 0)
+        for e in range(1, E // N):
+            for pair in range(PAIRS):
+                values_pair(0, pair, e, take(2))
+        quantise(("wk", 0, 0))
+
+        vector_work = [lambda: interleave_weight("wk", 1, 0), lambda: quantise(("wk", 1, 0)),
+                       lambda: interleave_weight("wk", 0, 1), lambda: interleave_weight("wk", 1, 1),
+                       lambda: quantise(("wk", 0, 1)), lambda: quantise(("wk", 1, 1))]
+        for i in range(TILES):
+            values_rows(1, i, take(E // N))
+            vector_work[i]()
+        for j in range(H // P - 1):
+            keys_rows(j, take(2))
+            if TILES + j < len(vector_work):
+                vector_work[TILES + j]()
+        for h in range(2):
+            keys_half_rows(H // P - 1, h, take(1)[0])

@@ -57,14 +57,30 @@ def tile_latent_key_value_cache_s9_kernel(tc, x, down_words, down_scales, gain, 
         ident = kept("ident", [P, P], F32)
         make_identity(nc, ident[:])
 
-        scale_raw = {}
-        for g0 in range(0, D_PASSES, SCALE_PASSES):
-            scale_raw[g0] = kept("scale_raw%d" % g0, [P, SCALE_PASSES * L // 4], I32)
-            nc.vector.memset(scale_raw[g0][:], 0)
         zero = kept("zero", [P, 1], F32)
         nc.vector.memset(zero[:], 0.0)
         rows32 = kept("rows32", [P, N], F32)
         nc.scalar.activation(out=rows32[:], in_=zero[:].to_broadcast([P, N]), func=IDENTITY)
+
+        scale_raw = {}
+        for g0 in range(0, D_PASSES, SCALE_PASSES):
+            scale_raw[g0] = kept("scale_raw%d" % g0, [P, SCALE_PASSES * L // 4], I32)
+            nc.vector.memset(scale_raw[g0][:], 0)
+
+        zeros = grouped_tile()[:, 0:KP]
+        idle_moving, idle_moving_scales = kept("idle_moving", [P, N], U32), kept("idle_moving_scales", [P, N], U8)
+        idle_fixed, idle_fixed_scales = kept("idle_fixed", [P, P], U32), kept("idle_fixed_scales", [P, P], U8)
+        nc.vector.memset(zeros.bitcast(I32), 0)
+        nc.vector.memset(idle_moving[:, P:], 0)
+        nc.vector.memset(idle_moving_scales[:, P:].bitcast(I32), 0)
+        nc.vector.quantize_mx(out=idle_moving[:, 0:P].bitcast(E5M2), scales=idle_moving_scales[:, 0:P], in_=zeros)
+        nc.vector.quantize_mx(out=idle_fixed[:].bitcast(E4M3), scales=idle_fixed_scales[:], in_=zeros)
+
+        def warm_passes(count, b):
+            sink = bank(b, [P, N])
+            for n in range(count):
+                nc.tensor.matmul_mx(out=sink[:], lhsT=idle_fixed[:].bitcast(E4M3), lhsT_scale=idle_fixed_scales[:],
+                                    rhs=idle_moving[:].bitcast(E5M2), rhs_scale=idle_moving_scales[:], start=True, stop=True)
 
         x_raw, w_raw, weight_raw = {}, {}, {}
 
@@ -274,12 +290,15 @@ def tile_latent_key_value_cache_s9_kernel(tc, x, down_words, down_scales, gain, 
             nc.sync.dma_start(out=keys[j * P:(j + 1) * P, h * N:(h + 1) * N], in_=out[:])
 
         sums, spare = [0, 1, 2, 3, 4, 5], [6, 7]
+        warm_passes(3, 0)
         for pair in range(PAIRS):
             sort_x(0, 0, (pair,))
             transpose_pair(0, 0, pair, spare[pair])
         empty_x(0, 0, scalar_copy)
+        warm_passes(3, 1)
         sort_x(0, 1, both)
         transpose_x(0, 1, sums[4:6])
+        warm_passes(1, 2)
         empty_x(0, 1, scalar_copy)
         for g in range(D_PASSES):
             if g == D_PASSES - 1:

from contextlib import ExitStack

import concourse.mybir as mybir
from concourse.masks import make_identity

T, D, L, H, E = 1024, 2048, 1024, 1024, 1536
FLOPS = 2 * T * D * L + 2 * T * L * (H + E)

F32 = mybir.dt.float32
BF16 = mybir.dt.bfloat16
I32 = mybir.dt.int32
U32 = mybir.dt.uint32
U8 = mybir.dt.uint8
E4M3 = mybir.dt.float8_e4m3fn_x4
E5M2 = mybir.dt.float8_e5m2_x4
E2M1 = mybir.dt.float4_e2m1fn_x4
IDENTITY = mybir.ActivationFunctionType.Identity
ADD = mybir.AluOpType.add

P = 128
PACK = 4
KP = P * PACK
N = 512
D_PASSES = D // KP
L_PASSES = L // KP
TILES = N // P
PAIRS = TILES // 2
RUN = 4
SCALE_PASSES = 2
SORTED_BUFS = 4
GROUPED_BUFS = 5
RESULT_BUFS = 7
BIAS_ROW = 32


def tile_latent_key_value_cache_s9_kernel(tc, x, down_words, down_scales, gain, shift, wk, bk, wv, keys, values):
    nc = tc.nc
    with ExitStack() as ctx:
        keep = ctx.enter_context(tc.tile_pool(name="keep", bufs=1))
        stage = ctx.enter_context(tc.tile_pool(name="stage", bufs=2))
        psum = ctx.enter_context(tc.psum_pool(name="psum", bufs=1))
        ctx.enter_context(tc.manual_schedule())
        scalar_copy, vector_copy = nc.scalar.copy, nc.vector.tensor_copy

        def kept(name, shape, dtype):
            return keep.tile(shape, dtype, name=name, align_bytes=64)

        def bank(b, shape):
            return psum.tile(shape, F32, name="bank%d" % b)

        def grouped_tile():
            return stage.tile([P, PACK * N], BF16, name="grouped", bufs=GROUPED_BUFS, align_bytes=64)

        def result_tile(shape, dtype):
            return stage.tile(shape, dtype, name="result", bufs=RESULT_BUFS)

        ident = kept("ident", [P, P], F32)
        make_identity(nc, ident[:])

        zero = kept("zero", [P, 1], F32)
        nc.vector.memset(zero[:], 0.0)
        rows32 = kept("rows32", [P, N], F32)
        nc.scalar.activation(out=rows32[:], in_=zero[:].to_broadcast([P, N]), func=IDENTITY)

        scale_raw = {}
        for g0 in range(0, D_PASSES, SCALE_PASSES):
            scale_raw[g0] = kept("scale_raw%d" % g0, [P, SCALE_PASSES * L // 4], I32)
            nc.vector.memset(scale_raw[g0][:], 0)

        zeros = grouped_tile()[:, 0:KP]
        idle_moving, idle_moving_scales = kept("idle_moving", [P, N], U32), kept("idle_moving_scales", [P, N], U8)
        idle_fixed, idle_fixed_scales = kept("idle_fixed", [P, P], U32), kept("idle_fixed_scales", [P, P], U8)
        nc.vector.memset(zeros.bitcast(I32), 0)
        nc.vector.memset(idle_moving[:, P:], 0)
        nc.vector.memset(idle_moving_scales[:, P:].bitcast(I32), 0)
        nc.vector.quantize_mx(out=idle_moving[:, 0:P].bitcast(E5M2), scales=idle_moving_scales[:, 0:P], in_=zeros)
        nc.vector.quantize_mx(out=idle_fixed[:].bitcast(E4M3), scales=idle_fixed_scales[:], in_=zeros)

        def warm_passes(count, b):
            sink = bank(b, [P, N])
            for n in range(count):
                nc.tensor.matmul_mx(out=sink[:], lhsT=idle_fixed[:].bitcast(E4M3), lhsT_scale=idle_fixed_scales[:],
                                    rhs=idle_moving[:].bitcast(E5M2), rhs_scale=idle_moving_scales[:], start=True, stop=True)

        x_raw, w_raw, weight_raw = {}, {}, {}

        def load_x(h, g0, g1, pairs):
            raw = kept("x_raw%d%d%d" % (h, g0, pairs[0]), [P, 2 * len(pairs), (g1 - g0) * KP], BF16)
            row = h * N + pairs[0] * 2 * P
            src = x[row:row + len(pairs) * 2 * P, g0 * KP:g1 * KP].rearrange("(i p) k -> p i k", p=P)
            nc.sync.dma_start(out=raw[:], in_=src)
            for g in range(g0, g1):
                x_raw[h, g, pairs] = raw[:, :, (g - g0) * KP:(g - g0 + 1) * KP]

        def load_w(g):
            w_raw[g] = result_tile([P, KP], I32)
            nc.sync.dma_start(out=w_raw[g][:], in_=down_words[g].bitcast(I32))

        def load_w_scales(g0):
            for r in range(4):
                nc.sync.dma_start(
                    out=scale_raw[g0][r:P:32, :].rearrange("q (g n) -> q g n", g=SCALE_PASSES),
                    in_=down_scales[g0:g0 + SCALE_PASSES, r:16:4, :].bitcast(I32).rearrange("g q n -> q g n"))

        rows16 = kept("rows16", [P, N], BF16)

        def load_channel_vectors():
            nc.sync.dma_start(out=rows16[0:2, :], in_=gain.rearrange("(c n) -> c n", n=N))
            nc.sync.dma_start(out=rows16[2:4, :], in_=shift.rearrange("(c n) -> c n", n=N))
            nc.sync.dma_start(out=rows16[BIAS_ROW:BIAS_ROW + 2, :], in_=bk.rearrange("(c n) -> c n", n=N))

        def load_weight(kind, c, e0, e1):
            weight = wk if kind == "wk" else wv
            raw = kept("%s_raw%d%d" % (kind, c, e0), [P, PACK, (e1 - e0) * N], BF16)
            rows = weight[c * KP:(c + 1) * KP, e0 * N:e1 * N].rearrange("(m t b) n -> b m t n", t=PACK, b=RUN)
            for b in range(RUN):
                nc.sync.dma_start(out=raw[b:P:RUN, :, :], in_=rows[b])
            for e in range(e0, e1):
                weight_raw[kind, c, e] = raw[:, :, (e - e0) * N:(e - e0 + 1) * N]

        both = tuple(range(PAIRS))
        load_x(0, 0, 1, (0,))
        load_x(0, 0, 1, (1,))
        load_x(0, 1, 2, both)
        load_w(0)
        load_w_scales(0)
        load_x(0, 2, 3, both)
        load_w(1)
        load_channel_vectors()
        load_x(0, 3, 4, both)
        load_w_scales(2)
        load_w(2)
        load_w(3)
        load_weight("wv", 0, 0, 2)
        load_x(1, 0, 2, both)
        load_x(1, 2, 4, both)
        load_weight("wv", 1, 0, 2)
        for c in range(L_PASSES):
            load_weight("wv", c, 2, 3)
        for c in range(L_PASSES):
            load_weight("wk", c, 0, 2)

        w_codes, w_scales = {}, {}

        def reorder_w_scales(g0):
            planes = kept("w_scales%d" % g0, [P, SCALE_PASSES * L], U8)
            nc.vector.tensor_copy(
                out=planes[:].bitcast(I32).rearrange("p (j t a i) -> p j a t i", j=SCALE_PASSES * L_PASSES, t=PACK, i=4),
                in_=scale_raw[g0][:].rearrange("p (j a i t) -> p j a t i", j=SCALE_PASSES * L_PASSES, t=PACK, i=4))
            for g in range(g0, g0 + SCALE_PASSES):
                for c in range(L_PASSES):
                    first = (g - g0) * L + c * KP
                    w_scales[c, g] = planes[:, first:first + KP]

        def reorder_w_codes(g):
            codes = kept("w_codes%d" % g, [P, 2 * L], U8)
            nc.vector.tensor_copy(
                out=codes[:].bitcast(I32).rearrange("p (c t m w) -> p c t m w", c=L_PASSES, t=PACK, w=2),
                in_=w_raw[g][:].rearrange("p (c m t w) -> p c t m w", c=L_PASSES, t=PACK, w=2))
            for c in range(L_PASSES):
                w_codes[c, g] = codes[:, c * 2 * KP:(c + 1) * 2 * KP]

        sorted_x, turned, grouped, quantised = {}, {}, {}, {}

        def sort_x(h, g, pairs):
            if pairs[0] == 0:
                sorted_x[h, g] = stage.tile([P, TILES, 2, P], F32, name="sorted_x", bufs=SORTED_BUFS, align_bytes=64)
            vector_copy(out=sorted_x[h, g][:, 2 * pairs[0]:2 * pairs[-1] + 2, :, :],
                        in_=x_raw[h, g, pairs].bitcast(F32).rearrange("p i (m u) -> p i u m", u=2))

        def transpose_pair(h, g, pair, b):
            turned[h, g, pair] = bank(b, [P, 2, 2, P])
            for i in range(2):
                for u in range(2):
                    nc.tensor.transpose(turned[h, g, pair][:, i, u, :], sorted_x[h, g][:, 2 * pair + i, u, :], ident[:])

        def transpose_x(h, g, banks):
            for pair in range(PAIRS):
                transpose_pair(h, g, pair, banks[pair])

        def empty_x(h, g, copy):
            grouped["x", h, g] = grouped_tile()
            for pair in range(PAIRS):
                dst = grouped["x", h, g][:, pair * 2 * N:(pair + 1) * 2 * N].bitcast(F32)
                copy(out=dst.rearrange("p (i r u) -> p i r u", i=2, u=2),
                     in_=turned[h, g, pair][:].rearrange("p i u r -> p i r u"))

        def interleave(key, src, copy):
            grouped[key] = grouped_tile()
            copy(out=grouped[key][:].rearrange("p (c i t) -> p c t i", t=PACK, i=4),
                 in_=src.rearrange("p t (c i) -> p c t i", i=4))

        def quantise(key, pieces=1):
            name = "%s_%d_%d" % key
            codes, scales = kept("codes_" + name, [P, N], U32), kept("scales_" + name, [P, N], U8)
            fmt = E5M2 if key[0] == "c" else E4M3
            width = N // pieces
            for n in range(pieces):
                cols = slice(n * width, (n + 1) * width)
                nc.vector.quantize_mx(out=codes[:, cols].bitcast(fmt), scales=scales[:, cols],
                                      in_=grouped[key][:, PACK * n * width:PACK * (n + 1) * width])
            quantised[key] = (codes, scales)

        def interleave_weight(kind, c, e):
            interleave((kind, c, e), weight_raw[kind, c, e], vector_copy)

        consts = kept("consts", [P, PACK, 2 * BIAS_ROW], F32)

        def widen_channel_vectors():
            scalar_copy(out=rows32[0:4, :].rearrange("p (t m b) -> p t m b", t=PACK, b=RUN),
                        in_=rows16[0:4, :].rearrange("p (m t b) -> p t m b", t=PACK, b=RUN))
            scalar_copy(out=rows32[BIAS_ROW:BIAS_ROW + 2, :], in_=rows16[BIAS_ROW:BIAS_ROW + 2, :])

        def transpose_channel_vectors(b):
            cols = bank(b, [P, PACK, P])
            for t in range(PACK):
                nc.tensor.transpose(cols[:, t, :], rows32[:, t * P:(t + 1) * P], ident[:])
            scalar_copy(out=consts[:], in_=cols[:, :, 0:2 * BIAS_ROW])

        z, latent = {}, {}

        def down_pass(h, c, t, g, b):
            if g == 0:
                z[h, c, t] = bank(b, [P, N])
            codes, scales = quantised["x", h, g]
            nc.tensor.matmul_mx(
                out=z[h, c, t][:],
                lhsT=w_codes[c, g][:, 2 * t * P:2 * (t + 1) * P].bitcast(E2M1),
                lhsT_scale=w_scales[c, g][:, t * P:(t + 1) * P],
                rhs=codes[:].bitcast(E4M3), rhs_scale=scales[:], start=(g == 0), stop=(g == D_PASSES - 1))

        def down_group(h, c, t, b):
            for g in range(D_PASSES):
                down_pass(h, c, t, g, b)

        def empty_z(h, c, t):
            if t == 0:
                latent[h, c] = stage.tile([P, PACK, N], BF16, name="latent", align_bytes=64)
            nc.scalar.activation(out=latent[h, c][:, t, :], in_=z[h, c, t][:], func=IDENTITY,
                                 scale=consts[:, t, c:c + 1], bias=consts[:, t, 2 + c:3 + c])

        def interleave_latent(h, c, copy):
            interleave(("c", h, c), latent[h, c][:], copy)

        def second_stage_group(b, fixed, fixed_fmt, cols, moving, moving_fmt):
            acc = bank(b, [P, N])
            for c in range(L_PASSES):
                (fixed_codes, fixed_scales), (moving_codes, moving_scales) = quantised[fixed(c)], quantised[moving(c)]
                nc.tensor.matmul_mx(out=acc[:], lhsT=fixed_codes[:, cols].bitcast(fixed_fmt), lhsT_scale=fixed_scales[:, cols],
                                    rhs=moving_codes[:].bitcast(moving_fmt), rhs_scale=moving_scales[:],
                                    start=(c == 0), stop=(c == L_PASSES - 1))
            return acc

        def values_block(h, i, e, b, out, copy):
            acc = second_stage_group(b, lambda c: ("c", h, c), E5M2, slice(i * P, (i + 1) * P), lambda c: ("wv", c, e), E4M3)
            copy(out=out, in_=acc[:])

        def keys_block(j, h, b, out):
            cols = slice((j % TILES) * P, (j % TILES + 1) * P)
            acc = second_stage_group(b, lambda c: ("wk", c, j // TILES), E4M3, cols, lambda c: ("c", h, c), E5M2)
            bias = consts[:, j % PACK, BIAS_ROW + j // PACK:BIAS_ROW + j // PACK + 1]
            if h == 0:
                nc.vector.tensor_scalar(out=out, in0=acc[:], scalar1=bias, scalar2=None, op0=ADD)
            else:
                nc.scalar.activation(out=out, in_=acc[:], func=IDENTITY, bias=bias)

        def values_pair(h, pair, e, banks):
            out = result_tile([P, 2, N], F32)
            for n in range(2):
                values_block(h, 2 * pair + n, e, banks[n], out[:, n, :], scalar_copy)
            row = h * N + 2 * pair * P
            nc.sync.dma_start(out=values[row:row + 2 * P, e * N:(e + 1) * N].rearrange("(i p) n -> p i n", p=P), in_=out[:])

        def values_rows(h, i, banks):
            out = result_tile([P, E], F32)
            for e in range(E // N):
                values_block(h, i, e, banks[e], out[:, e * N:(e + 1) * N], vector_copy if e == 0 else scalar_copy)
            row = h * N + i * P
            nc.sync.dma_start(out=values[row:row + P, :], in_=out[:])

        def keys_rows(j, banks):
            out = result_tile([P, T], F32)
            for h in range(2):
                keys_block(j, h, banks[h], out[:, h * N:(h + 1) * N])
            nc.sync.dma_start(out=keys[j * P:(j + 1) * P, :], in_=out[:])

        def keys_half_rows(j, h, b):
            out = result_tile([P, N], F32)
            keys_block(j, h, b, out[:])
            nc.sync.dma_start(out=keys[j * P:(j + 1) * P, h * N:(h + 1) * N], in_=out[:])

        sums, spare = [0, 1, 2, 3, 4, 5], [6, 7]
        warm_passes(3, 0)
        for pair in range(PAIRS):
            sort_x(0, 0, (pair,))
            transpose_pair(0, 0, pair, spare[pair])
        empty_x(0, 0, scalar_copy)
        warm_passes(3, 1)
        sort_x(0, 1, both)
        transpose_x(0, 1, sums[4:6])
        warm_passes(1, 2)
        empty_x(0, 1, scalar_copy)
        for g in range(D_PASSES):
            if g == D_PASSES - 1:
                reorder_w_codes(g)
                transpose_channel_vectors(spare[0])
            quantise(("x", 0, g), PAIRS)
            if g % SCALE_PASSES == 0:
                reorder_w_scales(g)
            if g < D_PASSES - 1:
                reorder_w_codes(g)
            for n, b in enumerate(sums):
                down_pass(0, n // PACK, n % PACK, g, b)
            if g + 2 < D_PASSES:
                sort_x(0, g + 2, both)
                transpose_x(0, g + 2, spare)
                if g + 2 == D_PASSES - 1:
                    widen_channel_vectors()
                empty_x(0, g + 2, scalar_copy)

        for t in range(PACK):
            empty_z(0, 0, t)
        interleave_weight("wv", 0, 0)
        interleave_weight("wv", 0, 1)
        sort_x(1, 0, both)
        sort_x(1, 1, both)
        quantise(("wv", 0, 0))
        down_group(0, 1, 2, spare[1])
        empty_z(0, 1, 0)
        empty_z(0, 1, 1)
        transpose_x(1, 0, sums[0:2])
        transpose_x(1, 1, sums[2:4])
        empty_x(1, 0, vector_copy)
        empty_x(1, 1, scalar_copy)
        sort_x(1, 2, both)
        sort_x(1, 3, both)
        down_group(0, 1, 3, spare[0])
        empty_z(0, 1, 2)
        transpose_x(1, 2, sums[4:6])
        transpose_x(1, 3, [spare[1], sums[0]])
        empty_z(0, 1, 3)
        quantise(("x", 1, 0))
        quantise(("x", 1, 1))
        quantise(("wv", 0, 1))
        empty_x(1, 2, scalar_copy)
        empty_x(1, 3, scalar_copy)
        quantise(("x", 1, 2))
        interleave_latent(0, 0, vector_copy)
        quantise(("x", 1, 3))
        interleave_latent(0, 1, scalar_copy)

        ring = [sums[1], sums[2], sums[3], spare[0], sums[4], sums[5], spare[1], sums[0]]
        for g in range(D_PASSES):
            for t in range(PACK):
                down_pass(1, 0, t, g, ring[t])
        for t in range(PACK):
            empty_z(1, 0, t)
        quantise(("c", 0, 0))
        interleave_weight("wv", 1, 0)
        quantise(("c", 0, 1))
        quantise(("wv", 1, 0))
        interleave_weight("wv", 1, 1)
        interleave_weight("wv", 0, 2)
        quantise(("wv", 1, 1))
        interleave_weight("wv", 1, 2)
        quantise(("wv", 0, 2))
        quantise(("wv", 1, 2))
        interleave_latent(1, 0, vector_copy)

        free = ring[PACK:] + ring[:PACK]

        def take(count):
            taken = free[:count]
            free[:] = free[count:] + taken
            return taken

        for t in range(PACK):
            down_group(1, 1, t, take(1)[0])
            empty_z(1, 1, t)
            if t in (1, 2):
                values_pair(0, t - 1, 0, take(2))
        interleave_latent(1, 1, vector_copy)
        quantise(("c", 1, 0))
        quantise(("c", 1, 1))
        interleave_weight("wk", 0, 0)
        for e in range(1, E // N):
            for pair in range(PAIRS):
                values_pair(0, pair, e, take(2))
        quantise(("wk", 0, 0))

        vector_work = [lambda: interleave_weight("wk", 1, 0), lambda: quantise(("wk", 1, 0)),
                       lambda: interleave_weight("wk", 0, 1), lambda: interleave_weight("wk", 1, 1),
                       lambda: quantise(("wk", 0, 1)), lambda: quantise(("wk", 1, 1))]
        for i in range(TILES):
            values_rows(1, i, take(E // N))
            vector_work[i]()
        for j in range(H // P - 1):
            keys_rows(j, take(2))
            if TILES + j < len(vector_work):
                vector_work[TILES + j]()
        for h in range(2):
            keys_half_rows(H // P - 1, h, take(1)[0])
